import numpy as np
import ml_dtypes


def mxq(x, axis, fmt="e4m3"):
    dtype, down = {"e4m3": (ml_dtypes.float8_e4m3fn, 7), "e5m2": (ml_dtypes.float8_e5m2, 14)}[fmt]
    v = np.moveaxis(np.asarray(x, np.float32).astype(ml_dtypes.bfloat16).astype(np.float64), axis, -1)
    blocks = v.reshape(v.shape[:-1] + (-1, 32))
    amax = np.abs(blocks).max(-1, keepdims=True)
    byte = np.maximum(np.where(amax > 0, np.frexp(amax)[1] - 1 + 127, 0) - down, 1)
    scale = np.exp2(byte - 127.0)
    codes = (blocks / scale).astype(np.float32).astype(dtype).astype(np.float64)
    return np.moveaxis((codes * scale).reshape(v.shape), -1, axis)


WIDE = False


def mx_kscale(k):
    if not WIDE:
        return np.ones(k)
    levels = np.array([10, -10, 5, -5, 0])
    if k % 512:
        return np.exp2(np.random.permutation(np.resize(levels, k // 32))).repeat(32)
    a = np.empty((k // 512, 16))
    for p in range(k // 512):
        a[p, :8] = np.random.permutation(np.resize(levels, 8))
        for g in range(8):
            far = levels[np.abs(levels - a[p, g]) >= 10]
            a[p, g + 8] = far[np.random.randint(len(far))]
    return np.exp2(a.ravel()).repeat(32)


def f64(x):
    return np.asarray(x).astype(np.float64)


def striped(idx):
    return np.tile(idx.reshape(-1, 16).T, (8, 1)).astype(np.uint16)


def unstriped(offs):
    return offs[:16].T.reshape(-1).astype(np.int64)


def striped8(idx):
    return np.concatenate([x.reshape(-1, 16).T for x in idx]).astype(np.uint16)


def runs(offs, k):
    lists = np.stack([offs[16 * r : 16 * r + 16].T.reshape(-1) for r in range(8)]).astype(np.int64)
    return lists[np.arange(k) % 512 // 64]


def pack_weight(w):
    k, n = w.shape
    w = f64(np.asarray(w, np.float32).astype(ml_dtypes.bfloat16)).reshape(k // 32, 32, n)
    amax = np.abs(w).max(1)
    byte = np.clip(np.where(amax > 0, np.frexp(amax)[1] - 1 + 127 - 7, 1), 1, 254)
    scaled = (w * np.exp2(127.0 - byte)[:, None, :]).reshape(k, n).astype(np.float32)
    words = np.ascontiguousarray(scaled.reshape(k // 512, 128, 4, n).transpose(0, 1, 3, 2)).astype(ml_dtypes.float8_e4m3fn).view(np.uint8)
    return words, np.ascontiguousarray(byte.astype(np.uint8).reshape(k // 512, 16, n))


def unpack_weight(words, scales):
    g, p, n, _ = words.shape
    vals = np.ascontiguousarray(words).view(ml_dtypes.float8_e4m3fn).astype(np.float64) * np.repeat(np.exp2(scales.astype(np.float64) - 127.0), 8, axis=1)[..., None]
    return vals.transpose(0, 1, 3, 2).reshape(g * 512, n)


def relu(v):
    return np.maximum(v, 0.0)


K, T, S, V, N, H = 512, 2048, 512, 256, 512, 512


def setup_inputs():
    n = np.random.standard_normal
    s = mx_kscale(K)[:, None]
    u = mx_kscale(H)
    packed_xT = pack_weight(n((K, T)) * s)
    perm = np.stack([np.random.permutation(S) for _ in range(8)])
    return {
        "x_words": packed_xT[0],
        "x_scales": packed_xT[1],
        "w1": (n((K, H)) / np.sqrt(K) / s * u).astype(np.float32),
        "wa": np.repeat(np.random.uniform(0.3, 1.2, (8, V)), 64, axis=0).astype(np.float32),
        "wb": np.repeat(np.random.uniform(0.3, 1.2, (8, V)), 64, axis=0).astype(np.float32),
        "w2": (n((H, N)) / np.sqrt(H) / u[:, None]).astype(np.float32),
        "offs": striped(np.random.permutation(T)[:S]),
        "la": striped8(perm[:, :V]),
        "lb": striped8(perm[:, V:]),
    }


def reference(x_words, x_scales, w1, wa, wb, w2, offs, la, lb):
    xq = unpack_weight(x_words, x_scales)[:, unstriped(offs)]
    y = mxq(f64(w1), 0, "e4m3").T @ xq
    b = (y[np.arange(H)[:, None], runs(lb, H)]) * f64(wb)
    a = (relu(y[np.arange(H)[:, None], runs(la, H)])) * f64(wa)
    p = np.zeros((H, S))
    p[np.arange(H)[:, None], runs(la, H)] = a
    z = p.copy()
    z[np.arange(H)[:, None], runs(lb, H)] = b
    return mxq(f64(w2), 0, "e4m3").T @ mxq(z, 0, "e4m3")

@@ -1,0 +1,186 @@
+from contextlib import ExitStack
+
+import concourse.mybir as mybir
+
+K, T, S, V, N, H = 512, 2048, 512, 256, 512, 512
+FLOPS = 2 * K * H * S + 2 * H * N * S
+BYTES = K * T + 16 * T + 4 * K * H + 4 * H * N + 2 * 4 * 8 * V + 2 * 128 * (S + 2 * V) // 16 + 4 * N * S
+
+F32 = mybir.dt.float32
+BF16 = mybir.dt.bfloat16
+I32 = mybir.dt.int32
+U32 = mybir.dt.uint32
+U16 = mybir.dt.uint16
+U8 = mybir.dt.uint8
+FP8X4 = mybir.dt.float8_e4m3fn_x4
+MULT = mybir.AluOpType.mult
+RELU = mybir.ActivationFunctionType.Relu
+COPY = mybir.ActivationFunctionType.Copy
+
+P = 128
+PACK = 4
+HALF = S // 2
+W1_SPLIT = 64
+PLANE_ORDER = (0, 2, 3, 1)
+
+
+def tile_picked_tworoute_relu_p_kernel(
+    tc, x_words, x_scales, w1, wa, wb, w2, offs, la, lb, out
+):
+    nc = tc.nc
+    with ExitStack() as ctx:
+        lists = ctx.enter_context(tc.tile_pool(name="lists", bufs=1))
+        sb = ctx.enter_context(tc.tile_pool(name="sb", bufs=1))
+        psum = ctx.enter_context(tc.psum_pool(name="psum", bufs=1))
+
+        offs_sb = lists.tile([P, S // 16], U16, name="offs_sb")
+        la_sb = lists.tile([P, V // 16], U16, name="la_sb")
+        lb_sb = lists.tile([P, V // 16], U16, name="lb_sb")
+
+        xs_all = sb.tile([P, T], U8, name="xs_all", align_bytes=64)
+        nc.gpsimd.memset(xs_all[:].bitcast(I32), 0)
+        nc.sync.dma_start(offs_sb[:], offs)
+        w1_raw = sb.tile([P, PACK, H], F32, name="w1_raw", tag="stage_a", align_bytes=64)
+        nc.sync.dma_start(w1_raw[:], w1.rearrange("(p j) c -> p j c", j=PACK))
+        for q in range(4):
+            nc.sync.dma_start(
+                xs_all[32 * q : 32 * q + 4, :].bitcast(I32),
+                x_scales[0, 4 * q : 4 * q + 4, :].bitcast(I32),
+            )
+        xw_all = sb.tile([P, T], I32, name="xw_all", tag="stage_b", align_bytes=64)
+        nc.sync.dma_start(xw_all[:], x_words[0].rearrange("p n t -> p (n t)").bitcast(I32))
+        nc.sync.dma_start(lb_sb[:], lb)
+        nc.sync.dma_start(la_sb[:], la)
+
+        w1_bf = sb.tile([P, PACK, P, PACK], BF16, name="w1_bf", align_bytes=64)
+        w1_dst = w1_bf[:].rearrange("p t m j -> p m j t")
+        w1_src = w1_raw[:].rearrange("p j (m t) -> p m j t", t=PACK)
+        nc.vector.tensor_copy(w1_dst[:, :W1_SPLIT], w1_src[:, :W1_SPLIT])
+        nc.scalar.activation(w1_dst[:, W1_SPLIT:], w1_src[:, W1_SPLIT:], COPY)
+        xs = sb.tile([P, S], U8, name="xs", align_bytes=64)
+        nc.vector.tensor_copy(xs[:], xs_all[:].indirect(offs_sb[:]))
+
+        w1_codes = sb.tile([P, H], U32, name="w1_codes", align_bytes=64)
+        w1_scales = sb.tile([P, H], U8, name="w1_scales", align_bytes=64)
+        nc.vector.quantize_mx(
+            out=w1_codes[:].bitcast(FP8X4),
+            scales=w1_scales[:],
+            in_=w1_bf[:].rearrange("p t m j -> p (t m j)"),
+        )
+
+        gates = sb.tile([P, 2, V], F32, name="gates", tag="stage_a", align_bytes=64)
+        nc.sync.dma_start(gates[:, 1, :], wb.rearrange("(p j) v -> p j v", j=PACK)[:, 0, :])
+        nc.sync.dma_start(gates[:, 0, :], wa.rearrange("(p j) v -> p j v", j=PACK)[:, 0, :])
+
+        xw = sb.tile([P, S], U32, name="xw", align_bytes=64)
+        for h in range(2):
+            nc.vector.tensor_copy(
+                xw[:, h * HALF : (h + 1) * HALF],
+                xw_all[:].bitcast(U32).indirect(offs_sb[:, h * HALF // 16 : (h + 1) * HALF // 16]),
+            )
+
+        w2_raw = sb.tile([P, PACK, N], F32, name="w2_raw", tag="stage_b", align_bytes=64)
+        nc.sync.dma_start(w2_raw[:], w2.rearrange("(p j) c -> p j c", j=PACK))
+
+        def first_product(t, cols, bank):
+            acc = psum.tile([P, cols.stop - cols.start], F32, name="acc1", tag="bank%d" % bank)
+            nc.tensor.matmul_mx(
+                out=acc[:],
+                lhsT=w1_codes[:, t * P : (t + 1) * P].bitcast(FP8X4),
+                lhsT_scale=w1_scales[:, t * P : (t + 1) * P],
+                rhs=xw[:, cols].bitcast(FP8X4),
+                rhs_scale=xs[:, cols],
+                start=True,
+                stop=True,
+            )
+            return acc
+
+        y, y_pos = {}, {}
+        for t in PLANE_ORDER:
+            y[t] = sb.tile([P, S], F32, name="y%d" % t)
+            y_pos[t] = sb.tile([P, S], F32, name="y_pos%d" % t)
+        first = PLANE_ORDER[0]
+        lo, hi = slice(0, HALF), slice(HALF, S)
+        acc_lo = first_product(first, lo, 0)
+        acc_hi = first_product(first, hi, 1)
+        nc.scalar.copy(y[first][:, lo], acc_lo[:])
+        nc.vector.tensor_copy(y[first][:, hi], acc_hi[:])
+        nc.scalar.activation(y_pos[first][:, lo], acc_lo[:], RELU)
+        nc.scalar.activation(y_pos[first][:, hi], acc_hi[:], RELU)
+        for n, t in enumerate(PLANE_ORDER[1:]):
+            acc = first_product(t, slice(0, S), 2 + n)
+            nc.scalar.copy(y[t][:], acc[:])
+            nc.scalar.activation(y_pos[t][:], acc[:], RELU)
+
+        w2_bf = sb.tile([P, N, PACK], BF16, name="w2_bf", align_bytes=64)
+        nc.scalar.copy(
+            w2_bf[:].rearrange("p (c i) j -> p c j i", i=4),
+            w2_raw[:].rearrange("p j (c i) -> p c j i", i=4),
+        )
+        w2_codes = sb.tile([P, N], U32, name="w2_codes", align_bytes=64)
+        w2_scales = sb.tile([P, N], U8, name="w2_scales", align_bytes=64)
+
+        z_bf = [sb.tile([P, HALF, PACK], BF16, name="z_bf%d" % h, align_bytes=64) for h in range(2)]
+        picked_a, picked_b = {}, {}
+
+        def fetch_b(t):
+            picked_b[t] = sb.tile([P, V], F32, name="picked_b%d" % t)
+            nc.vector.tensor_copy(picked_b[t][:], y[t][:].indirect(lb_sb[:]))
+
+        def fetch_a(t):
+            picked_a[t] = sb.tile([P, V], F32, name="picked_a%d" % t)
+            nc.vector.tensor_copy(picked_a[t][:], y_pos[t][:].indirect(la_sb[:]))
+
+        fetch_b(first)
+        fetch_a(first)
+        for n, t in enumerate(PLANE_ORDER):
+            last = n == PACK - 1
+            z = sb.tile([P, S], F32, name="z", tag="z%d" % (n % (PACK - 1)))
+            nc.vector.tensor_tensor(z[:].indirect(lb_sb[:]), picked_b[t][:], gates[:, 1, :], MULT)
+            if last:
+                nc.vector.quantize_mx(
+                    out=w2_codes[:].bitcast(FP8X4),
+                    scales=w2_scales[:],
+                    in_=w2_bf[:].rearrange("p c j -> p (c j)"),
+                )
+            else:
+                fetch_b(PLANE_ORDER[n + 1])
+            nc.vector.tensor_tensor(z[:].indirect(la_sb[:]), picked_a[t][:], gates[:, 0, :], MULT)
+            if last:
+                nc.vector.tensor_copy(z_bf[0][:, :, t], z[:, lo])
+            else:
+                fetch_a(PLANE_ORDER[n + 1])
+                nc.scalar.copy(z_bf[0][:, :, t], z[:, lo])
+            nc.scalar.copy(z_bf[1][:, :, t], z[:, hi])
+
+        z_codes, z_scales = [], []
+        for h in range(2):
+            z_codes.append(sb.tile([P, HALF], U32, name="z_codes%d" % h, align_bytes=64))
+            z_scales.append(sb.tile([P, HALF], U8, name="z_scales%d" % h, align_bytes=64))
+            nc.vector.quantize_mx(
+                out=z_codes[h][:].bitcast(FP8X4),
+                scales=z_scales[h][:],
+                in_=z_bf[h][:].rearrange("p c j -> p (c j)"),
+            )
+
+        out_rows = out.rearrange("(r p) n -> p r n", p=P)
+        for h in range(2):
+            for pair in range(2):
+                res = sb.tile([P, 2, HALF], F32, name="res%d%d" % (h, pair))
+                for e in range(2):
+                    r = 2 * pair + e
+                    acc = psum.tile([P, HALF], F32, name="acc2", tag="bank%d" % ((5 + 4 * h + r) % 8))
+                    nc.tensor.matmul_mx(
+                        out=acc[:],
+                        lhsT=w2_codes[:, r * P : (r + 1) * P].bitcast(FP8X4),
+                        lhsT_scale=w2_scales[:, r * P : (r + 1) * P],
+                        rhs=z_codes[h][:].bitcast(FP8X4),
+                        rhs_scale=z_scales[h][:],
+                        start=True,
+                        stop=True,
+                    )
+                    if e == 0:
+                        nc.scalar.copy(res[:, e, :], acc[:])
+                    else:
+                        nc.vector.tensor_copy(res[:, e, :], acc[:])
+                nc.sync.dma_start(out_rows[:, 2 * pair : 2 * pair + 2, h * HALF : (h + 1) * HALF], res[:])

@@ -37,7 +37,7 @@ def tile_picked_tworoute_relu_p_kernel(
         la_sb = lists.tile([P, V // 16], U16, name="la_sb")
         lb_sb = lists.tile([P, V // 16], U16, name="lb_sb")
 
-        xs_all = sb.tile([P, T], U8, name="xs_all", align_bytes=64)
+        xs_all = sb.tile([P, T], U8, name="xs_all", tag="stage_c", align_bytes=64)
         nc.gpsimd.memset(xs_all[:].bitcast(I32), 0)
         nc.sync.dma_start(offs_sb[:], offs)
         w1_raw = sb.tile([P, PACK, H], F32, name="w1_raw", tag="stage_a", align_bytes=64)
@@ -60,17 +60,25 @@ def tile_picked_tworoute_relu_p_kernel(
         xs = sb.tile([P, S], U8, name="xs", align_bytes=64)
         nc.vector.tensor_copy(xs[:], xs_all[:].indirect(offs_sb[:]))
 
-        w1_codes = sb.tile([P, H], U32, name="w1_codes", align_bytes=64)
-        w1_scales = sb.tile([P, H], U8, name="w1_scales", align_bytes=64)
-        nc.vector.quantize_mx(
-            out=w1_codes[:].bitcast(FP8X4),
-            scales=w1_scales[:],
-            in_=w1_bf[:].rearrange("p t m j -> p (t m j)"),
-        )
+        w1_codes, w1_scales = {}, {}
 
-        gates = sb.tile([P, 2, V], F32, name="gates", tag="stage_a", align_bytes=64)
-        nc.sync.dma_start(gates[:, 1, :], wb.rearrange("(p j) v -> p j v", j=PACK)[:, 0, :])
-        nc.sync.dma_start(gates[:, 0, :], wa.rearrange("(p j) v -> p j v", j=PACK)[:, 0, :])
+        def quantize_w1(planes, tag):
+            width = len(planes) * P
+            codes = sb.tile([P, width], U32, name="w1_codes", tag=tag, align_bytes=64)
+            scales = sb.tile([P, width], U8, name="w1_scales%d" % planes[0], align_bytes=64)
+            nc.vector.quantize_mx(
+                out=codes[:].bitcast(FP8X4),
+                scales=scales[:],
+                in_=w1_bf[:, planes[0] : planes[-1] + 1].rearrange("p t m j -> p (t m j)"),
+            )
+            for n, t in enumerate(planes):
+                w1_codes[t] = codes[:, n * P : (n + 1) * P]
+                w1_scales[t] = scales[:, n * P : (n + 1) * P]
+
+        quantize_w1((0, 1), "w1_codes_early")
+
+        w2_raw = sb.tile([P, PACK, N], F32, name="w2_raw", tag="stage_a", align_bytes=64)
+        nc.sync.dma_start(w2_raw[:], w2.rearrange("(p j) c -> p j c", j=PACK))
 
         xw = sb.tile([P, S], U32, name="xw", align_bytes=64)
         for h in range(2):
@@ -79,15 +87,18 @@ def tile_picked_tworoute_relu_p_kernel(
                 xw_all[:].bitcast(U32).indirect(offs_sb[:, h * HALF // 16 : (h + 1) * HALF // 16]),
             )
 
-        w2_raw = sb.tile([P, PACK, N], F32, name="w2_raw", tag="stage_b", align_bytes=64)
-        nc.sync.dma_start(w2_raw[:], w2.rearrange("(p j) c -> p j c", j=PACK))
+        quantize_w1((2, 3), "stage_b")
+
+        gates = sb.tile([P, 2, V], F32, name="gates", tag="stage_c", align_bytes=64)
+        nc.sync.dma_start(gates[:, 1, :], wb.rearrange("(p j) v -> p j v", j=PACK)[:, 0, :])
+        nc.sync.dma_start(gates[:, 0, :], wa.rearrange("(p j) v -> p j v", j=PACK)[:, 0, :])
 
         def first_product(t, cols, bank):
             acc = psum.tile([P, cols.stop - cols.start], F32, name="acc1", tag="bank%d" % bank)
             nc.tensor.matmul_mx(
                 out=acc[:],
-                lhsT=w1_codes[:, t * P : (t + 1) * P].bitcast(FP8X4),
-                lhsT_scale=w1_scales[:, t * P : (t + 1) * P],
+                lhsT=w1_codes[t].bitcast(FP8X4),
+                lhsT_scale=w1_scales[t],
                 rhs=xw[:, cols].bitcast(FP8X4),
                 rhs_scale=xs[:, cols],
                 start=True,
@@ -97,14 +108,14 @@ def tile_picked_tworoute_relu_p_kernel(
 
         y, y_pos = {}, {}
         for t in PLANE_ORDER:
-            y[t] = sb.tile([P, S], F32, name="y%d" % t)
-            y_pos[t] = sb.tile([P, S], F32, name="y_pos%d" % t)
+            y[t] = sb.tile([P, S], F32, name="y", tag="y%d" % t, align_bytes=64)
+            y_pos[t] = sb.tile([P, S], F32, name="y_pos", tag="y_pos%d" % t, align_bytes=64)
         first = PLANE_ORDER[0]
         lo, hi = slice(0, HALF), slice(HALF, S)
         acc_lo = first_product(first, lo, 0)
         acc_hi = first_product(first, hi, 1)
         nc.scalar.copy(y[first][:, lo], acc_lo[:])
-        nc.vector.tensor_copy(y[first][:, hi], acc_hi[:])
+        nc.scalar.copy(y[first][:, hi], acc_hi[:])
         nc.scalar.activation(y_pos[first][:, lo], acc_lo[:], RELU)
         nc.scalar.activation(y_pos[first][:, hi], acc_hi[:], RELU)
         for n, t in enumerate(PLANE_ORDER[1:]):
@@ -112,7 +123,7 @@ def tile_picked_tworoute_relu_p_kernel(
             nc.scalar.copy(y[t][:], acc[:])
             nc.scalar.activation(y_pos[t][:], acc[:], RELU)
 
-        w2_bf = sb.tile([P, N, PACK], BF16, name="w2_bf", align_bytes=64)
+        w2_bf = sb.tile([P, N, PACK], BF16, name="w2_bf", tag="w2_bf", align_bytes=64)
         nc.scalar.copy(
             w2_bf[:].rearrange("p (c i) j -> p c j i", i=4),
             w2_raw[:].rearrange("p j (c i) -> p c j i", i=4),
@@ -131,27 +142,39 @@ def tile_picked_tworoute_relu_p_kernel(
             picked_a[t] = sb.tile([P, V], F32, name="picked_a%d" % t)
             nc.vector.tensor_copy(picked_a[t][:], y_pos[t][:].indirect(la_sb[:]))
 
-        fetch_b(first)
-        fetch_a(first)
-        for n, t in enumerate(PLANE_ORDER):
-            last = n == PACK - 1
-            z = sb.tile([P, S], F32, name="z", tag="z%d" % (n % (PACK - 1)))
-            nc.vector.tensor_tensor(z[:].indirect(lb_sb[:]), picked_b[t][:], gates[:, 1, :], MULT)
-            if last:
-                nc.vector.quantize_mx(
-                    out=w2_codes[:].bitcast(FP8X4),
-                    scales=w2_scales[:],
-                    in_=w2_bf[:].rearrange("p c j -> p (c j)"),
-                )
+        for t in PLANE_ORDER:
+            fetch_b(t)
+            fetch_a(t)
+
+        pa, pb, pc, pd = PLANE_ORDER
+        z_tag = {pa: "y%d" % pc, pb: "y_pos%d" % pc, pc: "y%d" % pc, pd: "w2_bf"}
+        z = {}
+
+        def put_b(t):
+            z[t] = sb.tile([P, S], F32, name="z", tag=z_tag[t], align_bytes=64)
+            nc.vector.tensor_tensor(z[t][:].indirect(lb_sb[:]), picked_b[t][:], gates[:, 1, :], MULT)
+
+        def put_a(t):
+            nc.vector.tensor_tensor(z[t][:].indirect(la_sb[:]), picked_a[t][:], gates[:, 0, :], MULT)
+            if t == pd:
+                nc.vector.tensor_copy(z_bf[0][:, :, t], z[t][:, lo])
             else:
-                fetch_b(PLANE_ORDER[n + 1])
-            nc.vector.tensor_tensor(z[:].indirect(la_sb[:]), picked_a[t][:], gates[:, 0, :], MULT)
-            if last:
-                nc.vector.tensor_copy(z_bf[0][:, :, t], z[:, lo])
-            else:
-                fetch_a(PLANE_ORDER[n + 1])
-                nc.scalar.copy(z_bf[0][:, :, t], z[:, lo])
-            nc.scalar.copy(z_bf[1][:, :, t], z[:, hi])
+                nc.scalar.copy(z_bf[0][:, :, t], z[t][:, lo])
+            nc.scalar.copy(z_bf[1][:, :, t], z[t][:, hi])
+
+        put_b(pa)
+        put_b(pb)
+        put_a(pa)
+        put_a(pb)
+        nc.vector.quantize_mx(
+            out=w2_codes[:].bitcast(FP8X4),
+            scales=w2_scales[:],
+            in_=w2_bf[:].rearrange("p c j -> p (c j)"),
+        )
+        put_b(pc)
+        put_b(pd)
+        put_a(pc)
+        put_a(pd)
 
         z_codes, z_scales = [], []
         for h in range(2):
@@ -163,24 +186,21 @@ def tile_picked_tworoute_relu_p_kernel(
                 in_=z_bf[h][:].rearrange("p c j -> p (c j)"),
             )
 
-        out_rows = out.rearrange("(r p) n -> p r n", p=P)
         for h in range(2):
-            for pair in range(2):
-                res = sb.tile([P, 2, HALF], F32, name="res%d%d" % (h, pair))
-                for e in range(2):
-                    r = 2 * pair + e
-                    acc = psum.tile([P, HALF], F32, name="acc2", tag="bank%d" % ((5 + 4 * h + r) % 8))
-                    nc.tensor.matmul_mx(
-                        out=acc[:],
-                        lhsT=w2_codes[:, r * P : (r + 1) * P].bitcast(FP8X4),
-                        lhsT_scale=w2_scales[:, r * P : (r + 1) * P],
-                        rhs=z_codes[h][:].bitcast(FP8X4),
-                        rhs_scale=z_scales[h][:],
-                        start=True,
-                        stop=True,
-                    )
-                    if e == 0:
-                        nc.scalar.copy(res[:, e, :], acc[:])
-                    else:
-                        nc.vector.tensor_copy(res[:, e, :], acc[:])
-                nc.sync.dma_start(out_rows[:, 2 * pair : 2 * pair + 2, h * HALF : (h + 1) * HALF], res[:])
+            for r in range(N // P):
+                acc = psum.tile([P, HALF], F32, name="acc2", tag="bank%d" % ((5 + 4 * h + r) % 8))
+                nc.tensor.matmul_mx(
+                    out=acc[:],
+                    lhsT=w2_codes[:, r * P : (r + 1) * P].bitcast(FP8X4),
+                    lhsT_scale=w2_scales[:, r * P : (r + 1) * P],
+                    rhs=z_codes[h][:].bitcast(FP8X4),
+                    rhs_scale=z_scales[h][:],
+                    start=True,
+                    stop=True,
+                )
+                res = sb.tile([P, HALF], F32, name="res", tag="res%d%d" % (h, r))
+                if r % 2 == 0:
+                    nc.scalar.copy(res[:], acc[:])
+                else:
+                    nc.vector.tensor_copy(res[:], acc[:])
+                nc.sync.dma_start(out[r * P : (r + 1) * P, h * HALF : (h + 1) * HALF], res[:])

@@ -22,6 +22,7 @@ PACK = 4
 HALF = S // 2
 W1_SPLIT = 64
 PLANE_ORDER = (0, 2, 3, 1)
+LAST_SPLIT = 160
 
 
 def tile_picked_tworoute_relu_p_kernel(
@@ -31,6 +32,8 @@ def tile_picked_tworoute_relu_p_kernel(
     with ExitStack() as ctx:
         lists = ctx.enter_context(tc.tile_pool(name="lists", bufs=1))
         sb = ctx.enter_context(tc.tile_pool(name="sb", bufs=1))
+        reused = ctx.enter_context(tc.tile_pool(name="reused", bufs=1))
+        staging = ctx.enter_context(tc.tile_pool(name="staging", bufs=1))
         psum = ctx.enter_context(tc.psum_pool(name="psum", bufs=1))
 
         offs_sb = lists.tile([P, S // 16], U16, name="offs_sb")
@@ -40,7 +43,7 @@ def tile_picked_tworoute_relu_p_kernel(
         xs_all = sb.tile([P, T], U8, name="xs_all", tag="stage_c", align_bytes=64)
         nc.gpsimd.memset(xs_all[:].bitcast(I32), 0)
         nc.sync.dma_start(offs_sb[:], offs)
-        w1_raw = sb.tile([P, PACK, H], F32, name="w1_raw", tag="stage_a", align_bytes=64)
+        w1_raw = staging.tile([P, PACK, H], F32, name="w1_raw", align_bytes=64, offset=0)
         nc.sync.dma_start(w1_raw[:], w1.rearrange("(p j) c -> p j c", j=PACK))
         for q in range(4):
             nc.sync.dma_start(
@@ -77,7 +80,10 @@ def tile_picked_tworoute_relu_p_kernel(
 
         quantize_w1((0, 1), "w1_codes_early")
 
-        w2_raw = sb.tile([P, PACK, N], F32, name="w2_raw", tag="stage_a", align_bytes=64)
+        gates = sb.tile([P, 2, V], F32, name="gates", tag="stage_c", align_bytes=64)
+        nc.sync.dma_start(gates[:, 1, :], wb.rearrange("(p j) v -> p j v", j=PACK)[:, 0, :])
+        nc.sync.dma_start(gates[:, 0, :], wa.rearrange("(p j) v -> p j v", j=PACK)[:, 0, :])
+        w2_raw = staging.tile([P, PACK, N], F32, name="w2_raw", align_bytes=64, offset=0)
         nc.sync.dma_start(w2_raw[:], w2.rearrange("(p j) c -> p j c", j=PACK))
 
         xw = sb.tile([P, S], U32, name="xw", align_bytes=64)
@@ -88,10 +94,6 @@ def tile_picked_tworoute_relu_p_kernel(
             )
 
         quantize_w1((2, 3), "stage_b")
-
-        gates = sb.tile([P, 2, V], F32, name="gates", tag="stage_c", align_bytes=64)
-        nc.sync.dma_start(gates[:, 1, :], wb.rearrange("(p j) v -> p j v", j=PACK)[:, 0, :])
-        nc.sync.dma_start(gates[:, 0, :], wa.rearrange("(p j) v -> p j v", j=PACK)[:, 0, :])
 
         def first_product(t, cols, bank):
             acc = psum.tile([P, cols.stop - cols.start], F32, name="acc1", tag="bank%d" % bank)
@@ -106,75 +108,96 @@ def tile_picked_tworoute_relu_p_kernel(
             )
             return acc
 
-        y, y_pos = {}, {}
+        pa, pb, pc, pd = PLANE_ORDER
+        lo, hi = slice(0, HALF), slice(HALF, S)
+        y = {}
         for t in PLANE_ORDER:
             y[t] = sb.tile([P, S], F32, name="y", tag="y%d" % t, align_bytes=64)
-            y_pos[t] = sb.tile([P, S], F32, name="y_pos", tag="y_pos%d" % t, align_bytes=64)
-        first = PLANE_ORDER[0]
-        lo, hi = slice(0, HALF), slice(HALF, S)
-        acc_lo = first_product(first, lo, 0)
-        acc_hi = first_product(first, hi, 1)
-        nc.scalar.copy(y[first][:, lo], acc_lo[:])
-        nc.scalar.copy(y[first][:, hi], acc_hi[:])
-        nc.scalar.activation(y_pos[first][:, lo], acc_lo[:], RELU)
-        nc.scalar.activation(y_pos[first][:, hi], acc_hi[:], RELU)
+        acc_lo = first_product(pa, lo, 0)
+        acc_hi = first_product(pa, hi, 1)
+        nc.scalar.copy(y[pa][:, lo], acc_lo[:])
+        nc.scalar.copy(y[pa][:, hi], acc_hi[:])
         for n, t in enumerate(PLANE_ORDER[1:]):
             acc = first_product(t, slice(0, S), 2 + n)
             nc.scalar.copy(y[t][:], acc[:])
-            nc.scalar.activation(y_pos[t][:], acc[:], RELU)
 
-        w2_bf = sb.tile([P, N, PACK], BF16, name="w2_bf", tag="w2_bf", align_bytes=64)
+        picked_a, picked_b, active_a = {}, {}, {}
+        for t in PLANE_ORDER:
+            picked_b[t] = sb.tile([P, V], F32, name="picked_b", tag="picked_b%d" % t, align_bytes=64)
+            nc.vector.tensor_copy(picked_b[t][:], y[t][:].indirect(lb_sb[:]))
+            if t == pa:
+                picked_a[t] = reused.tile([P, V], F32, name="picked_a_first", align_bytes=64, offset=0)
+            else:
+                picked_a[t] = sb.tile([P, V], F32, name="picked_a%d" % t, align_bytes=64)
+            nc.vector.tensor_copy(picked_a[t][:], y[t][:].indirect(la_sb[:]))
+
+        def activate(t):
+            if t in (pb, pc):
+                at = 6144 if t == pb else 7168
+                active_a[t] = staging.tile([P, V], F32, name="active_a%d" % t, align_bytes=64, offset=at)
+            else:
+                active_a[t] = sb.tile([P, V], F32, name="active_a%d" % t, align_bytes=64)
+            nc.scalar.activation(active_a[t][:], picked_a[t][:], RELU)
+
+        activate(pa)
+        w2_bf = sb.tile([P, N, PACK], BF16, name="w2_bf", align_bytes=64)
         nc.scalar.copy(
             w2_bf[:].rearrange("p (c i) j -> p c j i", i=4),
             w2_raw[:].rearrange("p j (c i) -> p c j i", i=4),
         )
-        w2_codes = sb.tile([P, N], U32, name="w2_codes", align_bytes=64)
-        w2_scales = sb.tile([P, N], U8, name="w2_scales", align_bytes=64)
+        for t in PLANE_ORDER[1:]:
+            activate(t)
 
-        z_bf = [sb.tile([P, HALF, PACK], BF16, name="z_bf%d" % h, align_bytes=64) for h in range(2)]
-        picked_a, picked_b = {}, {}
-
-        def fetch_b(t):
-            picked_b[t] = sb.tile([P, V], F32, name="picked_b%d" % t)
-            nc.vector.tensor_copy(picked_b[t][:], y[t][:].indirect(lb_sb[:]))
-
-        def fetch_a(t):
-            picked_a[t] = sb.tile([P, V], F32, name="picked_a%d" % t)
-            nc.vector.tensor_copy(picked_a[t][:], y_pos[t][:].indirect(la_sb[:]))
-
-        for t in PLANE_ORDER:
-            fetch_b(t)
-            fetch_a(t)
-
-        pa, pb, pc, pd = PLANE_ORDER
-        z_tag = {pa: "y%d" % pc, pb: "y_pos%d" % pc, pc: "y%d" % pc, pd: "w2_bf"}
+        z_bf = [
+            staging.tile([P, HALF, PACK], BF16, name="z_bf%d" % h, align_bytes=64, offset=2048 * h) for h in range(2)
+        ]
         z = {}
 
         def put_b(t):
-            z[t] = sb.tile([P, S], F32, name="z", tag=z_tag[t], align_bytes=64)
+            if t == pa:
+                z[t] = reused.tile([P, S], F32, name="z_first", align_bytes=64, offset=0)
+            elif t == pd:
+                z[t] = reused.tile([P, S], F32, name="z_last", align_bytes=64, offset=N // 2)
+            elif t == pc:
+                z[t] = staging.tile([P, S], F32, name="z_third", align_bytes=64, offset=4096)
+            else:
+                z[t] = sb.tile([P, S], F32, name="z_second", tag="y%d" % pd, align_bytes=64)
             nc.vector.tensor_tensor(z[t][:].indirect(lb_sb[:]), picked_b[t][:], gates[:, 1, :], MULT)
 
         def put_a(t):
-            nc.vector.tensor_tensor(z[t][:].indirect(la_sb[:]), picked_a[t][:], gates[:, 0, :], MULT)
-            if t == pd:
-                nc.vector.tensor_copy(z_bf[0][:, :, t], z[t][:, lo])
-            else:
-                nc.scalar.copy(z_bf[0][:, :, t], z[t][:, lo])
+            nc.vector.tensor_tensor(z[t][:].indirect(la_sb[:]), active_a[t][:], gates[:, 0, :], MULT)
+
+        def round_plane(t):
+            nc.scalar.copy(z_bf[0][:, :, t], z[t][:, lo])
             nc.scalar.copy(z_bf[1][:, :, t], z[t][:, hi])
+
+        w2_codes, w2_scales = [], []
+
+        def quantize_w2(half, codes_tag, scales):
+            w2_codes.append(sb.tile([P, N // 2], U32, name="w2_codes", tag=codes_tag, align_bytes=64))
+            w2_scales.append(scales)
+            nc.vector.quantize_mx(
+                out=w2_codes[half][:].bitcast(FP8X4),
+                scales=w2_scales[half][:],
+                in_=w2_bf[:, half * N // 2 : (half + 1) * N // 2].rearrange("p c j -> p (c j)"),
+            )
 
         put_b(pa)
         put_b(pb)
         put_a(pa)
-        put_a(pb)
-        nc.vector.quantize_mx(
-            out=w2_codes[:].bitcast(FP8X4),
-            scales=w2_scales[:],
-            in_=w2_bf[:].rearrange("p c j -> p (c j)"),
-        )
+        round_plane(pa)
         put_b(pc)
-        put_b(pd)
+        put_a(pb)
+        round_plane(pb)
         put_a(pc)
+        round_plane(pc)
+        put_b(pd)
+        quantize_w2(0, "w2_codes_first", reused.tile([P, N // 2], U8, name="w2_scales_first", align_bytes=64, offset=0))
         put_a(pd)
+        quantize_w2(1, "picked_b%d" % pd, sb.tile([P, N // 2], U8, name="w2_scales_second", align_bytes=64))
+        for h in range(2):
+            nc.vector.tensor_copy(z_bf[h][:, :LAST_SPLIT, pd], z[pd][:, h * HALF : h * HALF + LAST_SPLIT])
+            nc.scalar.copy(z_bf[h][:, LAST_SPLIT:, pd], z[pd][:, h * HALF + LAST_SPLIT : (h + 1) * HALF])
 
         z_codes, z_scales = [], []
         for h in range(2):
@@ -186,21 +209,26 @@ def tile_picked_tworoute_relu_p_kernel(
                 in_=z_bf[h][:].rearrange("p c j -> p (c j)"),
             )
 
-        for h in range(2):
-            for r in range(N // P):
-                acc = psum.tile([P, HALF], F32, name="acc2", tag="bank%d" % ((5 + 4 * h + r) % 8))
+        for r in range(N // P):
+            rows = slice(r * P, (r + 1) * P)
+            w_cols = slice(r % 2 * P, (r % 2 + 1) * P)
+            res = sb.tile([P, S], F32, name="res", tag="res%d" % r)
+            for h, cols in enumerate((lo, hi)):
+                acc = psum.tile([P, HALF], F32, name="acc2", tag="bank%d" % ((5 + 2 * r + h) % 8))
                 nc.tensor.matmul_mx(
                     out=acc[:],
-                    lhsT=w2_codes[:, r * P : (r + 1) * P].bitcast(FP8X4),
-                    lhsT_scale=w2_scales[:, r * P : (r + 1) * P],
+                    lhsT=w2_codes[r // 2][:, w_cols].bitcast(FP8X4),
+                    lhsT_scale=w2_scales[r // 2][:, w_cols],
                     rhs=z_codes[h][:].bitcast(FP8X4),
                     rhs_scale=z_scales[h][:],
                     start=True,
                     stop=True,
                 )
-                res = sb.tile([P, HALF], F32, name="res", tag="res%d%d" % (h, r))
-                if r % 2 == 0:
-                    nc.scalar.copy(res[:], acc[:])
+                if h == 0:
+                    nc.scalar.copy(res[:, cols], acc[:])
                 else:
-                    nc.vector.tensor_copy(res[:], acc[:])
-                nc.sync.dma_start(out[r * P : (r + 1) * P, h * HALF : (h + 1) * HALF], res[:])
+                    nc.vector.tensor_copy(res[:, cols], acc[:])
+                if r == 0:
+                    nc.sync.dma_start(out[rows, cols], res[:, cols])
+            if r > 0:
+                nc.sync.dma_start(out[rows, :], res[:])

@@ -20,9 +20,8 @@ COPY = mybir.ActivationFunctionType.Copy
 P = 128
 PACK = 4
 HALF = S // 2
-W1_SPLIT = 64
+W1_SPLIT = 80
 PLANE_ORDER = (0, 2, 3, 1)
-LAST_SPLIT = 160
 
 
 def tile_picked_tworoute_relu_p_kernel(
@@ -43,49 +42,30 @@ def tile_picked_tworoute_relu_p_kernel(
         xs_all = sb.tile([P, T], U8, name="xs_all", tag="stage_c", align_bytes=64)
         nc.gpsimd.memset(xs_all[:].bitcast(I32), 0)
         nc.sync.dma_start(offs_sb[:], offs)
-        w1_raw = staging.tile([P, PACK, H], F32, name="w1_raw", align_bytes=64, offset=0)
-        nc.sync.dma_start(w1_raw[:], w1.rearrange("(p j) c -> p j c", j=PACK))
+        w1_rows = w1.rearrange("(p j) c -> p j c", j=PACK)
+        w1_early = staging.tile([P, 2, H], F32, name="w1_early", align_bytes=64, offset=0)
+        nc.sync.dma_start(w1_early[:], w1_rows[:, :2])
         for q in range(4):
             nc.sync.dma_start(
                 xs_all[32 * q : 32 * q + 4, :].bitcast(I32),
                 x_scales[0, 4 * q : 4 * q + 4, :].bitcast(I32),
             )
-        xw_all = sb.tile([P, T], I32, name="xw_all", tag="stage_b", align_bytes=64)
+        xw_all = sb.tile([P, T], I32, name="xw_all", align_bytes=64)
         nc.sync.dma_start(xw_all[:], x_words[0].rearrange("p n t -> p (n t)").bitcast(I32))
+        w1_late = staging.tile([P, 2, H], F32, name="w1_late", align_bytes=64, offset=4096)
+        nc.sync.dma_start(w1_late[:], w1_rows[:, 2:])
         nc.sync.dma_start(lb_sb[:], lb)
         nc.sync.dma_start(la_sb[:], la)
 
+        pa, pb, pc, pd = PLANE_ORDER
         w1_bf = sb.tile([P, PACK, P, PACK], BF16, name="w1_bf", align_bytes=64)
-        w1_dst = w1_bf[:].rearrange("p t m j -> p m j t")
-        w1_src = w1_raw[:].rearrange("p j (m t) -> p m j t", t=PACK)
-        nc.vector.tensor_copy(w1_dst[:, :W1_SPLIT], w1_src[:, :W1_SPLIT])
-        nc.scalar.activation(w1_dst[:, W1_SPLIT:], w1_src[:, W1_SPLIT:], COPY)
+        nc.scalar.activation(
+            w1_bf[:, :, :, :2].rearrange("p t m j -> p m j t"),
+            w1_early[:].rearrange("p j (m t) -> p m j t", t=PACK),
+            COPY,
+        )
         xs = sb.tile([P, S], U8, name="xs", align_bytes=64)
         nc.vector.tensor_copy(xs[:], xs_all[:].indirect(offs_sb[:]))
-
-        w1_codes, w1_scales = {}, {}
-
-        def quantize_w1(planes, tag):
-            width = len(planes) * P
-            codes = sb.tile([P, width], U32, name="w1_codes", tag=tag, align_bytes=64)
-            scales = sb.tile([P, width], U8, name="w1_scales%d" % planes[0], align_bytes=64)
-            nc.vector.quantize_mx(
-                out=codes[:].bitcast(FP8X4),
-                scales=scales[:],
-                in_=w1_bf[:, planes[0] : planes[-1] + 1].rearrange("p t m j -> p (t m j)"),
-            )
-            for n, t in enumerate(planes):
-                w1_codes[t] = codes[:, n * P : (n + 1) * P]
-                w1_scales[t] = scales[:, n * P : (n + 1) * P]
-
-        quantize_w1((0, 1), "w1_codes_early")
-
-        gates = sb.tile([P, 2, V], F32, name="gates", tag="stage_c", align_bytes=64)
-        nc.sync.dma_start(gates[:, 1, :], wb.rearrange("(p j) v -> p j v", j=PACK)[:, 0, :])
-        nc.sync.dma_start(gates[:, 0, :], wa.rearrange("(p j) v -> p j v", j=PACK)[:, 0, :])
-        w2_raw = staging.tile([P, PACK, N], F32, name="w2_raw", align_bytes=64, offset=0)
-        nc.sync.dma_start(w2_raw[:], w2.rearrange("(p j) c -> p j c", j=PACK))
-
         xw = sb.tile([P, S], U32, name="xw", align_bytes=64)
         for h in range(2):
             nc.vector.tensor_copy(
@@ -93,7 +73,30 @@ def tile_picked_tworoute_relu_p_kernel(
                 xw_all[:].bitcast(U32).indirect(offs_sb[:, h * HALF // 16 : (h + 1) * HALF // 16]),
             )
 
-        quantize_w1((2, 3), "stage_b")
+        late_src = w1_late[:].rearrange("p j (m t) -> p t m j", t=PACK)
+        nc.vector.tensor_copy(w1_bf[:, pa, :W1_SPLIT, 2:], late_src[:, pa, :W1_SPLIT])
+        nc.scalar.copy(w1_bf[:, pa, W1_SPLIT:, 2:], late_src[:, pa, W1_SPLIT:])
+        nc.vector.tensor_copy(w1_bf[:, pb, :, 2:], late_src[:, pb])
+        nc.scalar.copy(w1_bf[:, pc, :, 2:], late_src[:, pc])
+        nc.scalar.copy(w1_bf[:, pd, :, 2:], late_src[:, pd])
+
+        w1_codes, w1_scales = {}, {}
+        for t in PLANE_ORDER:
+            codes = sb.tile([P, P], U32, name="w1_codes%d" % t, align_bytes=64)
+            scales = sb.tile([P, P], U8, name="w1_scales%d" % t, align_bytes=64)
+            nc.vector.quantize_mx(
+                out=codes[:].bitcast(FP8X4),
+                scales=scales[:],
+                in_=w1_bf[:, t].rearrange("p m j -> p (m j)"),
+            )
+            w1_codes[t] = codes[:]
+            w1_scales[t] = scales[:]
+
+        gates = sb.tile([P, 2, V], F32, name="gates", tag="stage_c", align_bytes=64)
+        nc.sync.dma_start(gates[:, 1, :], wb.rearrange("(p j) v -> p j v", j=PACK)[:, 0, :])
+        nc.sync.dma_start(gates[:, 0, :], wa.rearrange("(p j) v -> p j v", j=PACK)[:, 0, :])
+        w2_raw = staging.tile([P, PACK, N], F32, name="w2_raw", align_bytes=64, offset=0)
+        nc.sync.dma_start(w2_raw[:], w2.rearrange("(p j) c -> p j c", j=PACK))
 
         def first_product(t, cols, bank):
             acc = psum.tile([P, cols.stop - cols.start], F32, name="acc1", tag="bank%d" % bank)
@@ -108,7 +111,6 @@ def tile_picked_tworoute_relu_p_kernel(
             )
             return acc
 
-        pa, pb, pc, pd = PLANE_ORDER
         lo, hi = slice(0, HALF), slice(HALF, S)
         y = {}
         for t in PLANE_ORDER:
@@ -195,40 +197,39 @@ def tile_picked_tworoute_relu_p_kernel(
         quantize_w2(0, "w2_codes_first", reused.tile([P, N // 2], U8, name="w2_scales_first", align_bytes=64, offset=0))
         put_a(pd)
         quantize_w2(1, "picked_b%d" % pd, sb.tile([P, N // 2], U8, name="w2_scales_second", align_bytes=64))
-        for h in range(2):
-            nc.vector.tensor_copy(z_bf[h][:, :LAST_SPLIT, pd], z[pd][:, h * HALF : h * HALF + LAST_SPLIT])
-            nc.scalar.copy(z_bf[h][:, LAST_SPLIT:, pd], z[pd][:, h * HALF + LAST_SPLIT : (h + 1) * HALF])
+        quarters = (slice(0, P), slice(P, HALF))
+        for cols in quarters:
+            nc.vector.tensor_copy(z_bf[0][:, cols, pd], z[pd][:, cols])
+        nc.scalar.copy(z_bf[1][:, :, pd], z[pd][:, hi])
 
-        z_codes, z_scales = [], []
+        z_codes = [sb.tile([P, HALF], U32, name="z_codes%d" % h, align_bytes=64) for h in range(2)]
+        z_scales = [sb.tile([P, HALF], U8, name="z_scales%d" % h, align_bytes=64) for h in range(2)]
+        pieces = (quarters, (slice(0, HALF),))
         for h in range(2):
-            z_codes.append(sb.tile([P, HALF], U32, name="z_codes%d" % h, align_bytes=64))
-            z_scales.append(sb.tile([P, HALF], U8, name="z_scales%d" % h, align_bytes=64))
-            nc.vector.quantize_mx(
-                out=z_codes[h][:].bitcast(FP8X4),
-                scales=z_scales[h][:],
-                in_=z_bf[h][:].rearrange("p c j -> p (c j)"),
-            )
-
-        for r in range(N // P):
-            rows = slice(r * P, (r + 1) * P)
-            w_cols = slice(r % 2 * P, (r % 2 + 1) * P)
-            res = sb.tile([P, S], F32, name="res", tag="res%d" % r)
-            for h, cols in enumerate((lo, hi)):
-                acc = psum.tile([P, HALF], F32, name="acc2", tag="bank%d" % ((5 + 2 * r + h) % 8))
-                nc.tensor.matmul_mx(
-                    out=acc[:],
-                    lhsT=w2_codes[r // 2][:, w_cols].bitcast(FP8X4),
-                    lhsT_scale=w2_scales[r // 2][:, w_cols],
-                    rhs=z_codes[h][:].bitcast(FP8X4),
-                    rhs_scale=z_scales[h][:],
-                    start=True,
-                    stop=True,
+            for cols in pieces[h]:
+                nc.vector.quantize_mx(
+                    out=z_codes[h][:, cols].bitcast(FP8X4),
+                    scales=z_scales[h][:, cols],
+                    in_=z_bf[h][:, cols].rearrange("p c j -> p (c j)"),
                 )
-                if h == 0:
-                    nc.scalar.copy(res[:, cols], acc[:])
+
+        for h in range(2):
+            for r in range(N // P):
+                w_cols = slice(r % 2 * P, (r % 2 + 1) * P)
+                acc = psum.tile([P, HALF], F32, name="acc2", tag="bank%d" % ((5 + 4 * h + r) % 8))
+                for cols in pieces[h]:
+                    nc.tensor.matmul_mx(
+                        out=acc[:, cols],
+                        lhsT=w2_codes[r // 2][:, w_cols].bitcast(FP8X4),
+                        lhsT_scale=w2_scales[r // 2][:, w_cols],
+                        rhs=z_codes[h][:, cols].bitcast(FP8X4),
+                        rhs_scale=z_scales[h][:, cols],
+                        start=True,
+                        stop=True,
+                    )
+                res = sb.tile([P, HALF], F32, name="res", tag="res%d%d" % (h, r))
+                if r % 2 == 0:
+                    nc.scalar.copy(res[:], acc[:])
                 else:
-                    nc.vector.tensor_copy(res[:, cols], acc[:])
-                if r == 0:
-                    nc.sync.dma_start(out[rows, cols], res[:, cols])
-            if r > 0:
-                nc.sync.dma_start(out[rows, :], res[:])
+                    nc.vector.tensor_copy(res[:], acc[:])
+                nc.sync.dma_start(out[r * P : (r + 1) * P, h * HALF : (h + 1) * HALF], res[:])

@@ -22,6 +22,7 @@ PACK = 4
 HALF = S // 2
 W1_SPLIT = 80
 PLANE_ORDER = (0, 2, 3, 1)
+LAST_SPLIT = 160
 
 
 def tile_picked_tworoute_relu_p_kernel(
@@ -40,16 +41,14 @@ def tile_picked_tworoute_relu_p_kernel(
         lb_sb = lists.tile([P, V // 16], U16, name="lb_sb")
 
         xs_all = sb.tile([P, T], U8, name="xs_all", tag="stage_c", align_bytes=64)
-        nc.gpsimd.memset(xs_all[:].bitcast(I32), 0)
+        nc.vector.memset(xs_all[:].bitcast(I32), 0)
+        xs = sb.tile([P, S], U8, name="xs", align_bytes=64)
+        nc.vector.memset(xs[:].bitcast(I32), 0)
         nc.sync.dma_start(offs_sb[:], offs)
         w1_rows = w1.rearrange("(p j) c -> p j c", j=PACK)
         w1_early = staging.tile([P, 2, H], F32, name="w1_early", align_bytes=64, offset=0)
         nc.sync.dma_start(w1_early[:], w1_rows[:, :2])
-        for q in range(4):
-            nc.sync.dma_start(
-                xs_all[32 * q : 32 * q + 4, :].bitcast(I32),
-                x_scales[0, 4 * q : 4 * q + 4, :].bitcast(I32),
-            )
+        nc.sync.dma_start(xs_all[0:P:8, :].bitcast(I32), x_scales[0].bitcast(I32))
         xw_all = sb.tile([P, T], I32, name="xw_all", align_bytes=64)
         nc.sync.dma_start(xw_all[:], x_words[0].rearrange("p n t -> p (n t)").bitcast(I32))
         w1_late = staging.tile([P, 2, H], F32, name="w1_late", align_bytes=64, offset=4096)
@@ -64,8 +63,12 @@ def tile_picked_tworoute_relu_p_kernel(
             w1_early[:].rearrange("p j (m t) -> p m j t", t=PACK),
             COPY,
         )
-        xs = sb.tile([P, S], U8, name="xs", align_bytes=64)
-        nc.vector.tensor_copy(xs[:], xs_all[:].indirect(offs_sb[:]))
+        xs_spread = sb.tile([P, S], U8, name="xs_spread", align_bytes=64)
+        nc.vector.tensor_copy(xs_spread[:], xs_all[:].indirect(offs_sb[:]))
+        for q in range(4):
+            nc.sync.dma_start(
+                xs[32 * q : 32 * q + 4, :].bitcast(I32), xs_spread[32 * q : 32 * q + 32 : 8, :].bitcast(I32)
+            )
         xw = sb.tile([P, S], U32, name="xw", align_bytes=64)
         for h in range(2):
             nc.vector.tensor_copy(
@@ -147,8 +150,8 @@ def tile_picked_tworoute_relu_p_kernel(
             w2_bf[:].rearrange("p (c i) j -> p c j i", i=4),
             w2_raw[:].rearrange("p j (c i) -> p c j i", i=4),
         )
-        for t in PLANE_ORDER[1:]:
-            activate(t)
+        activate(pb)
+        activate(pd)
 
         z_bf = [
             staging.tile([P, HALF, PACK], BF16, name="z_bf%d" % h, align_bytes=64, offset=2048 * h) for h in range(2)
@@ -159,7 +162,7 @@ def tile_picked_tworoute_relu_p_kernel(
             if t == pa:
                 z[t] = reused.tile([P, S], F32, name="z_first", align_bytes=64, offset=0)
             elif t == pd:
-                z[t] = reused.tile([P, S], F32, name="z_last", align_bytes=64, offset=N // 2)
+                z[t] = reused.tile([P, S], F32, name="z_last", align_bytes=64, offset=0)
             elif t == pc:
                 z[t] = staging.tile([P, S], F32, name="z_third", align_bytes=64, offset=4096)
             else:
@@ -175,9 +178,9 @@ def tile_picked_tworoute_relu_p_kernel(
 
         w2_codes, w2_scales = [], []
 
-        def quantize_w2(half, codes_tag, scales):
-            w2_codes.append(sb.tile([P, N // 2], U32, name="w2_codes", tag=codes_tag, align_bytes=64))
-            w2_scales.append(scales)
+        def quantize_w2(half, codes):
+            w2_codes.append(codes)
+            w2_scales.append(sb.tile([P, N // 2], U8, name="w2_scales%d" % half, align_bytes=64))
             nc.vector.quantize_mx(
                 out=w2_codes[half][:].bitcast(FP8X4),
                 scales=w2_scales[half][:],
@@ -188,48 +191,50 @@ def tile_picked_tworoute_relu_p_kernel(
         put_b(pb)
         put_a(pa)
         round_plane(pa)
+        activate(pc)
         put_b(pc)
         put_a(pb)
         round_plane(pb)
+        put_b(pd)
         put_a(pc)
         round_plane(pc)
-        put_b(pd)
-        quantize_w2(0, "w2_codes_first", reused.tile([P, N // 2], U8, name="w2_scales_first", align_bytes=64, offset=0))
         put_a(pd)
-        quantize_w2(1, "picked_b%d" % pd, sb.tile([P, N // 2], U8, name="w2_scales_second", align_bytes=64))
-        quarters = (slice(0, P), slice(P, HALF))
-        for cols in quarters:
-            nc.vector.tensor_copy(z_bf[0][:, cols, pd], z[pd][:, cols])
-        nc.scalar.copy(z_bf[1][:, :, pd], z[pd][:, hi])
-
-        z_codes = [sb.tile([P, HALF], U32, name="z_codes%d" % h, align_bytes=64) for h in range(2)]
-        z_scales = [sb.tile([P, HALF], U8, name="z_scales%d" % h, align_bytes=64) for h in range(2)]
-        pieces = (quarters, (slice(0, HALF),))
+        quantize_w2(0, staging.tile([P, N // 2], U32, name="w2_codes0", align_bytes=64, offset=7168))
         for h in range(2):
-            for cols in pieces[h]:
-                nc.vector.quantize_mx(
-                    out=z_codes[h][:, cols].bitcast(FP8X4),
-                    scales=z_scales[h][:, cols],
-                    in_=z_bf[h][:, cols].rearrange("p c j -> p (c j)"),
-                )
+            nc.vector.tensor_copy(z_bf[h][:, :LAST_SPLIT, pd], z[pd][:, h * HALF : h * HALF + LAST_SPLIT])
+            nc.scalar.copy(z_bf[h][:, LAST_SPLIT:, pd], z[pd][:, h * HALF + LAST_SPLIT : (h + 1) * HALF])
 
-        for h in range(2):
+        z_codes, z_scales = [], []
+
+        def quantize_z(h):
+            z_codes.append(sb.tile([P, HALF], U32, name="z_codes%d" % h, align_bytes=64))
+            z_scales.append(sb.tile([P, HALF], U8, name="z_scales%d" % h, align_bytes=64))
+            nc.vector.quantize_mx(
+                out=z_codes[h][:].bitcast(FP8X4),
+                scales=z_scales[h][:],
+                in_=z_bf[h][:].rearrange("p c j -> p (c j)"),
+            )
+
+        quantize_z(0)
+        quantize_w2(1, reused.tile([P, N // 2], U32, name="w2_codes1", align_bytes=64, offset=0))
+        quantize_z(1)
+
+        for h, cols in enumerate((lo, hi)):
             for r in range(N // P):
                 w_cols = slice(r % 2 * P, (r % 2 + 1) * P)
                 acc = psum.tile([P, HALF], F32, name="acc2", tag="bank%d" % ((5 + 4 * h + r) % 8))
-                for cols in pieces[h]:
-                    nc.tensor.matmul_mx(
-                        out=acc[:, cols],
-                        lhsT=w2_codes[r // 2][:, w_cols].bitcast(FP8X4),
-                        lhsT_scale=w2_scales[r // 2][:, w_cols],
-                        rhs=z_codes[h][:, cols].bitcast(FP8X4),
-                        rhs_scale=z_scales[h][:, cols],
-                        start=True,
-                        stop=True,
-                    )
+                nc.tensor.matmul_mx(
+                    out=acc[:],
+                    lhsT=w2_codes[r // 2][:, w_cols].bitcast(FP8X4),
+                    lhsT_scale=w2_scales[r // 2][:, w_cols],
+                    rhs=z_codes[h][:].bitcast(FP8X4),
+                    rhs_scale=z_scales[h][:],
+                    start=True,
+                    stop=True,
+                )
                 res = sb.tile([P, HALF], F32, name="res", tag="res%d%d" % (h, r))
                 if r % 2 == 0:
                     nc.scalar.copy(res[:], acc[:])
                 else:
                     nc.vector.tensor_copy(res[:], acc[:])
-                nc.sync.dma_start(out[r * P : (r + 1) * P, h * HALF : (h + 1) * HALF], res[:])
+                nc.sync.dma_start(out[r * P : (r + 1) * P, cols], res[:])

@@ -20,9 +20,9 @@ COPY = mybir.ActivationFunctionType.Copy
 P = 128
 PACK = 4
 HALF = S // 2
-W1_SPLIT = 80
+RUN = 8
+W1_SPLIT = 10
 PLANE_ORDER = (0, 2, 3, 1)
-LAST_SPLIT = 160
 
 
 def tile_picked_tworoute_relu_p_kernel(
@@ -44,10 +44,10 @@ def tile_picked_tworoute_relu_p_kernel(
         nc.vector.memset(xs_all[:].bitcast(I32), 0)
         xs = sb.tile([P, S], U8, name="xs", align_bytes=64)
         nc.vector.memset(xs[:].bitcast(I32), 0)
-        nc.sync.dma_start(offs_sb[:], offs)
         w1_rows = w1.rearrange("(p j) c -> p j c", j=PACK)
         w1_early = staging.tile([P, 2, H], F32, name="w1_early", align_bytes=64, offset=0)
         nc.sync.dma_start(w1_early[:], w1_rows[:, :2])
+        nc.sync.dma_start(offs_sb[:], offs)
         nc.sync.dma_start(xs_all[0:P:8, :].bitcast(I32), x_scales[0].bitcast(I32))
         xw_all = sb.tile([P, T], I32, name="xw_all", align_bytes=64)
         nc.sync.dma_start(xw_all[:], x_words[0].rearrange("p n t -> p (n t)").bitcast(I32))
@@ -58,10 +58,9 @@ def tile_picked_tworoute_relu_p_kernel(
 
         pa, pb, pc, pd = PLANE_ORDER
         w1_bf = sb.tile([P, PACK, P, PACK], BF16, name="w1_bf", align_bytes=64)
-        nc.scalar.activation(
-            w1_bf[:, :, :, :2].rearrange("p t m j -> p m j t"),
-            w1_early[:].rearrange("p j (m t) -> p m j t", t=PACK),
-            COPY,
+        nc.scalar.copy(
+            w1_bf[:, :, :, :2].rearrange("p t (b r) j -> p b t r j", r=RUN),
+            w1_early[:].rearrange("p j (b t r) -> p b t r j", t=PACK, r=RUN),
         )
         xs_spread = sb.tile([P, S], U8, name="xs_spread", align_bytes=64)
         nc.vector.tensor_copy(xs_spread[:], xs_all[:].indirect(offs_sb[:]))
@@ -76,12 +75,13 @@ def tile_picked_tworoute_relu_p_kernel(
                 xw_all[:].bitcast(U32).indirect(offs_sb[:, h * HALF // 16 : (h + 1) * HALF // 16]),
             )
 
-        late_src = w1_late[:].rearrange("p j (m t) -> p t m j", t=PACK)
-        nc.vector.tensor_copy(w1_bf[:, pa, :W1_SPLIT, 2:], late_src[:, pa, :W1_SPLIT])
-        nc.scalar.copy(w1_bf[:, pa, W1_SPLIT:, 2:], late_src[:, pa, W1_SPLIT:])
-        nc.vector.tensor_copy(w1_bf[:, pb, :, 2:], late_src[:, pb])
-        nc.scalar.copy(w1_bf[:, pc, :, 2:], late_src[:, pc])
-        nc.scalar.copy(w1_bf[:, pd, :, 2:], late_src[:, pd])
+        late_src = w1_late[:].rearrange("p j (b t r) -> p t b r j", t=PACK, r=RUN)
+        late_dst = w1_bf[:, :, :, 2:].rearrange("p t (b r) j -> p t b r j", r=RUN)
+        nc.vector.tensor_copy(late_dst[:, pa, :W1_SPLIT], late_src[:, pa, :W1_SPLIT])
+        nc.scalar.copy(late_dst[:, pa, W1_SPLIT:], late_src[:, pa, W1_SPLIT:])
+        nc.vector.tensor_copy(late_dst[:, pb], late_src[:, pb])
+        nc.scalar.copy(late_dst[:, pc], late_src[:, pc])
+        nc.scalar.copy(late_dst[:, pd], late_src[:, pd])
 
         w1_codes, w1_scales = {}, {}
         for t in PLANE_ORDER:
@@ -96,10 +96,12 @@ def tile_picked_tworoute_relu_p_kernel(
             w1_scales[t] = scales[:]
 
         gates = sb.tile([P, 2, V], F32, name="gates", tag="stage_c", align_bytes=64)
-        nc.sync.dma_start(gates[:, 1, :], wb.rearrange("(p j) v -> p j v", j=PACK)[:, 0, :])
-        nc.sync.dma_start(gates[:, 0, :], wa.rearrange("(p j) v -> p j v", j=PACK)[:, 0, :])
+        nc.sync.dma_start(gates[:, 1, :], wb.rearrange("(b t r) v -> t b r v", t=PACK, r=RUN)[0])
+        nc.sync.dma_start(gates[:, 0, :], wa.rearrange("(b t r) v -> t b r v", t=PACK, r=RUN)[0])
         w2_raw = staging.tile([P, PACK, N], F32, name="w2_raw", align_bytes=64, offset=0)
-        nc.sync.dma_start(w2_raw[:], w2.rearrange("(p j) c -> p j c", j=PACK))
+        w2_rows = w2.rearrange("(b t r) c -> t b r c", t=PACK, r=RUN)
+        for t in range(PACK):
+            nc.sync.dma_start(w2_raw[:, t, :], w2_rows[t])
 
         def first_product(t, cols, bank):
             acc = psum.tile([P, cols.stop - cols.start], F32, name="acc1", tag="bank%d" % bank)
@@ -118,12 +120,12 @@ def tile_picked_tworoute_relu_p_kernel(
         y = {}
         for t in PLANE_ORDER:
             y[t] = sb.tile([P, S], F32, name="y", tag="y%d" % t, align_bytes=64)
-        acc_lo = first_product(pa, lo, 0)
-        acc_hi = first_product(pa, hi, 1)
-        nc.scalar.copy(y[pa][:, lo], acc_lo[:])
-        nc.scalar.copy(y[pa][:, hi], acc_hi[:])
+        pieces = (lo, slice(HALF, HALF + P), slice(HALF + P, S))
+        for n, cols in enumerate(pieces):
+            acc = first_product(pa, cols, n)
+            nc.scalar.copy(y[pa][:, cols], acc[:])
         for n, t in enumerate(PLANE_ORDER[1:]):
-            acc = first_product(t, slice(0, S), 2 + n)
+            acc = first_product(t, slice(0, S), 3 + n)
             nc.scalar.copy(y[t][:], acc[:])
 
         picked_a, picked_b, active_a = {}, {}, {}
@@ -200,41 +202,46 @@ def tile_picked_tworoute_relu_p_kernel(
         round_plane(pc)
         put_a(pd)
         quantize_w2(0, staging.tile([P, N // 2], U32, name="w2_codes0", align_bytes=64, offset=7168))
-        for h in range(2):
-            nc.vector.tensor_copy(z_bf[h][:, :LAST_SPLIT, pd], z[pd][:, h * HALF : h * HALF + LAST_SPLIT])
-            nc.scalar.copy(z_bf[h][:, LAST_SPLIT:, pd], z[pd][:, h * HALF + LAST_SPLIT : (h + 1) * HALF])
+        q0, q1 = slice(0, P), slice(P, HALF)
+        for cols in (q0, q1):
+            nc.vector.tensor_copy(z_bf[0][:, cols, pd], z[pd][:, cols])
+        nc.scalar.copy(z_bf[1][:, :, pd], z[pd][:, hi])
 
-        z_codes, z_scales = [], []
+        z_codes = [sb.tile([P, HALF], U32, name="z_codes%d" % h, align_bytes=64) for h in range(2)]
+        z_scales = [sb.tile([P, HALF], U8, name="z_scales%d" % h, align_bytes=64) for h in range(2)]
 
-        def quantize_z(h):
-            z_codes.append(sb.tile([P, HALF], U32, name="z_codes%d" % h, align_bytes=64))
-            z_scales.append(sb.tile([P, HALF], U8, name="z_scales%d" % h, align_bytes=64))
+        def quantize_z(h, cols):
             nc.vector.quantize_mx(
-                out=z_codes[h][:].bitcast(FP8X4),
-                scales=z_scales[h][:],
-                in_=z_bf[h][:].rearrange("p c j -> p (c j)"),
+                out=z_codes[h][:, cols].bitcast(FP8X4),
+                scales=z_scales[h][:, cols],
+                in_=z_bf[h][:, cols].rearrange("p c j -> p (c j)"),
             )
 
-        quantize_z(0)
+        quantize_z(0, q0)
+        quantize_z(0, q1)
+        quantize_z(1, lo)
         quantize_w2(1, reused.tile([P, N // 2], U32, name="w2_codes1", align_bytes=64, offset=0))
-        quantize_z(1)
 
-        for h, cols in enumerate((lo, hi)):
-            for r in range(N // P):
-                w_cols = slice(r % 2 * P, (r % 2 + 1) * P)
-                acc = psum.tile([P, HALF], F32, name="acc2", tag="bank%d" % ((5 + 4 * h + r) % 8))
-                nc.tensor.matmul_mx(
-                    out=acc[:],
-                    lhsT=w2_codes[r // 2][:, w_cols].bitcast(FP8X4),
-                    lhsT_scale=w2_scales[r // 2][:, w_cols],
-                    rhs=z_codes[h][:].bitcast(FP8X4),
-                    rhs_scale=z_scales[h][:],
-                    start=True,
-                    stop=True,
-                )
-                res = sb.tile([P, HALF], F32, name="res", tag="res%d%d" % (h, r))
-                if r % 2 == 0:
-                    nc.scalar.copy(res[:], acc[:])
-                else:
-                    nc.vector.tensor_copy(res[:], acc[:])
-                nc.sync.dma_start(out[r * P : (r + 1) * P, cols], res[:])
+        res = [sb.tile([P, S], F32, name="res%d" % r, align_bytes=64) for r in range(N // P)]
+        units = [(0, 0, q0), (0, 0, q1), (1, 0, lo), (0, 1, lo), (1, 1, lo), (2, 0, lo), (2, 1, lo), (3, 0, lo), (3, 1, lo)]
+        for n, (r, h, cols) in enumerate(units):
+            w_cols = slice(r % 2 * P, (r % 2 + 1) * P)
+            acc = psum.tile([P, cols.stop - cols.start], F32, name="acc2", tag="bank%d" % ((6 + n) % 8))
+            nc.tensor.matmul_mx(
+                out=acc[:],
+                lhsT=w2_codes[r // 2][:, w_cols].bitcast(FP8X4),
+                lhsT_scale=w2_scales[r // 2][:, w_cols],
+                rhs=z_codes[h][:, cols].bitcast(FP8X4),
+                rhs_scale=z_scales[h][:, cols],
+                start=True,
+                stop=True,
+            )
+            tokens = slice(h * HALF + cols.start, h * HALF + cols.stop)
+            if n < 3 or n % 2 == 0:
+                nc.scalar.copy(res[r][:, tokens], acc[:])
+            else:
+                nc.vector.tensor_copy(res[r][:, tokens], acc[:])
+            if r != 2:
+                nc.sync.dma_start(out[r * P : (r + 1) * P, tokens], res[r][:, tokens])
+            elif h == 1:
+                nc.sync.dma_start(out[r * P : (r + 1) * P, :], res[r][:])

@@ -21,6 +21,7 @@ P = 128
 PACK = 4
 HALF = S // 2
 RUN = 8
+EARLY = 1
 W1_SPLIT = 10
 PLANE_ORDER = (0, 2, 3, 1)
 
@@ -41,33 +42,36 @@ def tile_picked_tworoute_relu_p_kernel(
         lb_sb = lists.tile([P, V // 16], U16, name="lb_sb")
 
         xs_all = sb.tile([P, T], U8, name="xs_all", tag="stage_c", align_bytes=64)
-        nc.vector.memset(xs_all[:].bitcast(I32), 0)
+        for rows in (slice(0, 16), slice(32, 64), slice(64, P)):
+            nc.vector.memset(xs_all[rows, :].bitcast(I32), 0)
         xs = sb.tile([P, S], U8, name="xs", align_bytes=64)
         nc.vector.memset(xs[:].bitcast(I32), 0)
         w1_rows = w1.rearrange("(p j) c -> p j c", j=PACK)
-        w1_early = staging.tile([P, 2, H], F32, name="w1_early", align_bytes=64, offset=0)
-        nc.sync.dma_start(w1_early[:], w1_rows[:, :2])
+        w1_early = staging.tile([P, EARLY, H], F32, name="w1_early", align_bytes=64, offset=0)
+        nc.sync.dma_start(w1_early[:], w1_rows[:, :EARLY])
         nc.sync.dma_start(offs_sb[:], offs)
-        nc.sync.dma_start(xs_all[0:P:8, :].bitcast(I32), x_scales[0].bitcast(I32))
+        nc.sync.dma_start(xs_all[16:32, :].bitcast(I32), x_scales[0].bitcast(I32))
         xw_all = sb.tile([P, T], I32, name="xw_all", align_bytes=64)
         nc.sync.dma_start(xw_all[:], x_words[0].rearrange("p n t -> p (n t)").bitcast(I32))
-        w1_late = staging.tile([P, 2, H], F32, name="w1_late", align_bytes=64, offset=4096)
-        nc.sync.dma_start(w1_late[:], w1_rows[:, 2:])
+        w1_late = staging.tile([P, PACK - EARLY, H], F32, name="w1_late", align_bytes=64, offset=4 * H * EARLY)
+        nc.sync.dma_start(w1_late[:], w1_rows[:, EARLY:])
         nc.sync.dma_start(lb_sb[:], lb)
         nc.sync.dma_start(la_sb[:], la)
 
         pa, pb, pc, pd = PLANE_ORDER
         w1_bf = sb.tile([P, PACK, P, PACK], BF16, name="w1_bf", align_bytes=64)
-        nc.scalar.copy(
-            w1_bf[:, :, :, :2].rearrange("p t (b r) j -> p b t r j", r=RUN),
-            w1_early[:].rearrange("p j (b t r) -> p b t r j", t=PACK, r=RUN),
-        )
+        early_src = w1_early[:, 0, :].rearrange("p (b t r) -> p t b r", t=PACK, r=RUN)
+        early_dst = w1_bf[:, :, :, 0].rearrange("p t (b r) -> p t b r", r=RUN)
+        nc.scalar.copy(early_dst[:, pa, W1_SPLIT:], early_src[:, pa, W1_SPLIT:])
+        nc.scalar.copy(early_dst[:, pd::2], early_src[:, pd::2])
         xs_spread = sb.tile([P, S], U8, name="xs_spread", align_bytes=64)
         nc.vector.tensor_copy(xs_spread[:], xs_all[:].indirect(offs_sb[:]))
         for q in range(4):
             nc.sync.dma_start(
-                xs[32 * q : 32 * q + 4, :].bitcast(I32), xs_spread[32 * q : 32 * q + 32 : 8, :].bitcast(I32)
+                xs[32 * q : 32 * q + 4, :].bitcast(I32), xs_spread[16 + 4 * q : 20 + 4 * q, :].bitcast(I32)
             )
+        nc.vector.tensor_copy(early_dst[:, pa, :W1_SPLIT], early_src[:, pa, :W1_SPLIT])
+        nc.vector.tensor_copy(early_dst[:, pb], early_src[:, pb])
         xw = sb.tile([P, S], U32, name="xw", align_bytes=64)
         for h in range(2):
             nc.vector.tensor_copy(
@@ -76,7 +80,7 @@ def tile_picked_tworoute_relu_p_kernel(
             )
 
         late_src = w1_late[:].rearrange("p j (b t r) -> p t b r j", t=PACK, r=RUN)
-        late_dst = w1_bf[:, :, :, 2:].rearrange("p t (b r) j -> p t b r j", r=RUN)
+        late_dst = w1_bf[:, :, :, EARLY:].rearrange("p t (b r) j -> p t b r j", r=RUN)
         nc.vector.tensor_copy(late_dst[:, pa, :W1_SPLIT], late_src[:, pa, :W1_SPLIT])
         nc.scalar.copy(late_dst[:, pa, W1_SPLIT:], late_src[:, pa, W1_SPLIT:])
         nc.vector.tensor_copy(late_dst[:, pb], late_src[:, pb])
@@ -123,7 +127,10 @@ def tile_picked_tworoute_relu_p_kernel(
         pieces = (lo, slice(HALF, HALF + P), slice(HALF + P, S))
         for n, cols in enumerate(pieces):
             acc = first_product(pa, cols, n)
-            nc.scalar.copy(y[pa][:, cols], acc[:])
+            if n == 1:
+                nc.vector.tensor_copy(y[pa][:, cols], acc[:])
+            else:
+                nc.scalar.copy(y[pa][:, cols], acc[:])
         for n, t in enumerate(PLANE_ORDER[1:]):
             acc = first_product(t, slice(0, S), 3 + n)
             nc.scalar.copy(y[t][:], acc[:])

@@ -42,15 +42,14 @@ def tile_picked_tworoute_relu_p_kernel(
         lb_sb = lists.tile([P, V // 16], U16, name="lb_sb")
 
         xs_all = sb.tile([P, T], U8, name="xs_all", tag="stage_c", align_bytes=64)
-        for rows in (slice(0, 16), slice(32, 64), slice(64, P)):
-            nc.vector.memset(xs_all[rows, :].bitcast(I32), 0)
+        nc.vector.memset(xs_all[: P - 16, :].bitcast(I32), 0)
         xs = sb.tile([P, S], U8, name="xs", align_bytes=64)
         nc.vector.memset(xs[:].bitcast(I32), 0)
         w1_rows = w1.rearrange("(p j) c -> p j c", j=PACK)
         w1_early = staging.tile([P, EARLY, H], F32, name="w1_early", align_bytes=64, offset=0)
         nc.sync.dma_start(w1_early[:], w1_rows[:, :EARLY])
         nc.sync.dma_start(offs_sb[:], offs)
-        nc.sync.dma_start(xs_all[16:32, :].bitcast(I32), x_scales[0].bitcast(I32))
+        nc.sync.dma_start(xs_all[P - 16 :, :].bitcast(I32), x_scales[0].bitcast(I32))
         xw_all = sb.tile([P, T], I32, name="xw_all", align_bytes=64)
         nc.sync.dma_start(xw_all[:], x_words[0].rearrange("p n t -> p (n t)").bitcast(I32))
         w1_late = staging.tile([P, PACK - EARLY, H], F32, name="w1_late", align_bytes=64, offset=4 * H * EARLY)
@@ -68,7 +67,7 @@ def tile_picked_tworoute_relu_p_kernel(
         nc.vector.tensor_copy(xs_spread[:], xs_all[:].indirect(offs_sb[:]))
         for q in range(4):
             nc.sync.dma_start(
-                xs[32 * q : 32 * q + 4, :].bitcast(I32), xs_spread[16 + 4 * q : 20 + 4 * q, :].bitcast(I32)
+                xs[32 * q : 32 * q + 4, :].bitcast(I32), xs_spread[P - 16 + 4 * q : P - 12 + 4 * q, :].bitcast(I32)
             )
         nc.vector.tensor_copy(early_dst[:, pa, :W1_SPLIT], early_src[:, pa, :W1_SPLIT])
         nc.vector.tensor_copy(early_dst[:, pb], early_src[:, pb])
@@ -230,7 +229,7 @@ def tile_picked_tworoute_relu_p_kernel(
         quantize_w2(1, reused.tile([P, N // 2], U32, name="w2_codes1", align_bytes=64, offset=0))
 
         res = [sb.tile([P, S], F32, name="res%d" % r, align_bytes=64) for r in range(N // P)]
-        units = [(0, 0, q0), (0, 0, q1), (1, 0, lo), (0, 1, lo), (1, 1, lo), (2, 0, lo), (2, 1, lo), (3, 0, lo), (3, 1, lo)]
+        units = [(0, 0, q0), (0, 0, q1), (1, 0, lo), (0, 1, lo), (1, 1, lo), (2, 0, lo), (2, 1, lo), (3, 0, lo), (3, 1, q0), (3, 1, q1)]
         for n, (r, h, cols) in enumerate(units):
             w_cols = slice(r % 2 * P, (r % 2 + 1) * P)
             acc = psum.tile([P, cols.stop - cols.start], F32, name="acc2", tag="bank%d" % ((6 + n) % 8))
@@ -248,7 +247,7 @@ def tile_picked_tworoute_relu_p_kernel(
                 nc.scalar.copy(res[r][:, tokens], acc[:])
             else:
                 nc.vector.tensor_copy(res[r][:, tokens], acc[:])
-            if r != 2:
+            if r < 2:
                 nc.sync.dma_start(out[r * P : (r + 1) * P, tokens], res[r][:, tokens])
-            elif h == 1:
+            elif tokens.stop == S:
                 nc.sync.dma_start(out[r * P : (r + 1) * P, :], res[r][:])

@@ -15,14 +15,18 @@ U8 = mybir.dt.uint8
 FP8X4 = mybir.dt.float8_e4m3fn_x4
 MULT = mybir.AluOpType.mult
 RELU = mybir.ActivationFunctionType.Relu
-COPY = mybir.ActivationFunctionType.Copy
 
 P = 128
 PACK = 4
-HALF = S // 2
 RUN = 8
-EARLY = 1
+LIST_ROWS = 16
+SCALE_ROWS = K // 32
+LINE = 4
+BANKS = 8
+HALF = S // 2
+ROW_BYTES = 4 * H
 W1_SPLIT = 10
+LAST_SPLIT = 160
 PLANE_ORDER = (0, 2, 3, 1)
 
 
@@ -37,54 +41,58 @@ def tile_picked_tworoute_relu_p_kernel(
         staging = ctx.enter_context(tc.tile_pool(name="staging", bufs=1))
         psum = ctx.enter_context(tc.psum_pool(name="psum", bufs=1))
 
-        offs_sb = lists.tile([P, S // 16], U16, name="offs_sb")
-        la_sb = lists.tile([P, V // 16], U16, name="la_sb")
-        lb_sb = lists.tile([P, V // 16], U16, name="lb_sb")
+        offs_sb = lists.tile([P, S // LIST_ROWS], U16, name="offs_sb")
+        la_sb = lists.tile([P, V // LIST_ROWS], U16, name="la_sb")
+        lb_sb = lists.tile([P, V // LIST_ROWS], U16, name="lb_sb")
 
+        scale_base = P - SCALE_ROWS
         xs_all = sb.tile([P, T], U8, name="xs_all", tag="stage_c", align_bytes=64)
-        nc.vector.memset(xs_all[: P - 16, :].bitcast(I32), 0)
+        nc.vector.memset(xs_all[:scale_base, :].bitcast(I32), 0)
         xs = sb.tile([P, S], U8, name="xs", align_bytes=64)
         nc.vector.memset(xs[:].bitcast(I32), 0)
+
         w1_rows = w1.rearrange("(p j) c -> p j c", j=PACK)
-        w1_early = staging.tile([P, EARLY, H], F32, name="w1_early", align_bytes=64, offset=0)
-        nc.sync.dma_start(w1_early[:], w1_rows[:, :EARLY])
+        w1_early = staging.tile([P, 1, H], F32, name="w1_early", align_bytes=64, offset=0)
+        nc.sync.dma_start(w1_early[:], w1_rows[:, :1])
         nc.sync.dma_start(offs_sb[:], offs)
-        nc.sync.dma_start(xs_all[P - 16 :, :].bitcast(I32), x_scales[0].bitcast(I32))
+        nc.sync.dma_start(xs_all[scale_base:, :].bitcast(I32), x_scales[0].bitcast(I32))
         xw_all = sb.tile([P, T], I32, name="xw_all", align_bytes=64)
         nc.sync.dma_start(xw_all[:], x_words[0].rearrange("p n t -> p (n t)").bitcast(I32))
-        w1_late = staging.tile([P, PACK - EARLY, H], F32, name="w1_late", align_bytes=64, offset=4 * H * EARLY)
-        nc.sync.dma_start(w1_late[:], w1_rows[:, EARLY:])
+        w1_late = staging.tile([P, PACK - 1, H], F32, name="w1_late", align_bytes=64, offset=ROW_BYTES)
+        nc.sync.dma_start(w1_late[:], w1_rows[:, 1:])
         nc.sync.dma_start(lb_sb[:], lb)
         nc.sync.dma_start(la_sb[:], la)
 
-        pa, pb, pc, pd = PLANE_ORDER
+        first, second, third, last = PLANE_ORDER
         w1_bf = sb.tile([P, PACK, P, PACK], BF16, name="w1_bf", align_bytes=64)
         early_src = w1_early[:, 0, :].rearrange("p (b t r) -> p t b r", t=PACK, r=RUN)
         early_dst = w1_bf[:, :, :, 0].rearrange("p t (b r) -> p t b r", r=RUN)
-        nc.scalar.copy(early_dst[:, pa, W1_SPLIT:], early_src[:, pa, W1_SPLIT:])
-        nc.scalar.copy(early_dst[:, pd::2], early_src[:, pd::2])
-        xs_spread = sb.tile([P, S], U8, name="xs_spread", align_bytes=64)
-        nc.vector.tensor_copy(xs_spread[:], xs_all[:].indirect(offs_sb[:]))
+        nc.scalar.copy(early_dst[:, first, W1_SPLIT:], early_src[:, first, W1_SPLIT:])
+        odd_planes = slice(last, PACK, third - last)
+        nc.scalar.copy(early_dst[:, odd_planes], early_src[:, odd_planes])
+
+        xs_picked = sb.tile([P, S], U8, name="xs_picked", align_bytes=64)
+        nc.vector.tensor_copy(xs_picked[:], xs_all[:].indirect(offs_sb[:]))
         for q in range(4):
-            nc.sync.dma_start(
-                xs[32 * q : 32 * q + 4, :].bitcast(I32), xs_spread[P - 16 + 4 * q : P - 12 + 4 * q, :].bitcast(I32)
-            )
-        nc.vector.tensor_copy(early_dst[:, pa, :W1_SPLIT], early_src[:, pa, :W1_SPLIT])
-        nc.vector.tensor_copy(early_dst[:, pb], early_src[:, pb])
+            rows = slice(scale_base + 4 * q, scale_base + 4 * q + 4)
+            nc.sync.dma_start(xs[32 * q : 32 * q + 4, :].bitcast(I32), xs_picked[rows, :].bitcast(I32))
+        nc.vector.tensor_copy(early_dst[:, first, :W1_SPLIT], early_src[:, first, :W1_SPLIT])
+        nc.vector.tensor_copy(early_dst[:, second], early_src[:, second])
+
         xw = sb.tile([P, S], U32, name="xw", align_bytes=64)
         for h in range(2):
             nc.vector.tensor_copy(
                 xw[:, h * HALF : (h + 1) * HALF],
-                xw_all[:].bitcast(U32).indirect(offs_sb[:, h * HALF // 16 : (h + 1) * HALF // 16]),
+                xw_all[:].bitcast(U32).indirect(offs_sb[:, h * HALF // LIST_ROWS : (h + 1) * HALF // LIST_ROWS]),
             )
 
         late_src = w1_late[:].rearrange("p j (b t r) -> p t b r j", t=PACK, r=RUN)
-        late_dst = w1_bf[:, :, :, EARLY:].rearrange("p t (b r) j -> p t b r j", r=RUN)
-        nc.vector.tensor_copy(late_dst[:, pa, :W1_SPLIT], late_src[:, pa, :W1_SPLIT])
-        nc.scalar.copy(late_dst[:, pa, W1_SPLIT:], late_src[:, pa, W1_SPLIT:])
-        nc.vector.tensor_copy(late_dst[:, pb], late_src[:, pb])
-        nc.scalar.copy(late_dst[:, pc], late_src[:, pc])
-        nc.scalar.copy(late_dst[:, pd], late_src[:, pd])
+        late_dst = w1_bf[:, :, :, 1:].rearrange("p t (b r) j -> p t b r j", r=RUN)
+        nc.vector.tensor_copy(late_dst[:, first, :W1_SPLIT], late_src[:, first, :W1_SPLIT])
+        nc.scalar.copy(late_dst[:, first, W1_SPLIT:], late_src[:, first, W1_SPLIT:])
+        nc.vector.tensor_copy(late_dst[:, second], late_src[:, second])
+        nc.scalar.copy(late_dst[:, third], late_src[:, third])
+        nc.scalar.copy(late_dst[:, last], late_src[:, last])
 
         w1_codes, w1_scales = {}, {}
         for t in PLANE_ORDER:
@@ -99,8 +107,9 @@ def tile_picked_tworoute_relu_p_kernel(
             w1_scales[t] = scales[:]
 
         gates = sb.tile([P, 2, V], F32, name="gates", tag="stage_c", align_bytes=64)
-        nc.sync.dma_start(gates[:, 1, :], wb.rearrange("(b t r) v -> t b r v", t=PACK, r=RUN)[0])
-        nc.sync.dma_start(gates[:, 0, :], wa.rearrange("(b t r) v -> t b r v", t=PACK, r=RUN)[0])
+        gate_a, gate_b = gates[:, 0, :], gates[:, 1, :]
+        nc.sync.dma_start(gate_b, wb.rearrange("(b t r) v -> t b r v", t=PACK, r=RUN)[0])
+        nc.sync.dma_start(gate_a, wa.rearrange("(b t r) v -> t b r v", t=PACK, r=RUN)[0])
         w2_raw = staging.tile([P, PACK, N], F32, name="w2_raw", align_bytes=64, offset=0)
         w2_rows = w2.rearrange("(b t r) c -> t b r c", t=PACK, r=RUN)
         for t in range(PACK):
@@ -123,62 +132,67 @@ def tile_picked_tworoute_relu_p_kernel(
         y = {}
         for t in PLANE_ORDER:
             y[t] = sb.tile([P, S], F32, name="y", tag="y%d" % t, align_bytes=64)
-        pieces = (lo, slice(HALF, HALF + P), slice(HALF + P, S))
-        for n, cols in enumerate(pieces):
-            acc = first_product(pa, cols, n)
-            if n == 1:
-                nc.vector.tensor_copy(y[pa][:, cols], acc[:])
-            else:
-                nc.scalar.copy(y[pa][:, cols], acc[:])
-        for n, t in enumerate(PLANE_ORDER[1:]):
-            acc = first_product(t, slice(0, S), 3 + n)
+        pieces = (
+            (lo, nc.scalar.copy),
+            (slice(HALF, HALF + P), nc.vector.tensor_copy),
+            (slice(HALF + P, S), nc.scalar.copy),
+        )
+        for bank, (cols, copy_out) in enumerate(pieces):
+            acc = first_product(first, cols, bank)
+            copy_out(y[first][:, cols], acc[:])
+        for bank, t in enumerate(PLANE_ORDER[1:], len(pieces)):
+            acc = first_product(t, slice(0, S), bank)
             nc.scalar.copy(y[t][:], acc[:])
+        banks_used = len(pieces) + PACK - 1
 
         picked_a, picked_b, active_a = {}, {}, {}
         for t in PLANE_ORDER:
             picked_b[t] = sb.tile([P, V], F32, name="picked_b", tag="picked_b%d" % t, align_bytes=64)
             nc.vector.tensor_copy(picked_b[t][:], y[t][:].indirect(lb_sb[:]))
-            if t == pa:
+            if t == first:
                 picked_a[t] = reused.tile([P, V], F32, name="picked_a_first", align_bytes=64, offset=0)
             else:
                 picked_a[t] = sb.tile([P, V], F32, name="picked_a%d" % t, align_bytes=64)
             nc.vector.tensor_copy(picked_a[t][:], y[t][:].indirect(la_sb[:]))
 
+        z_bf_at = (0, ROW_BYTES)
+        z_third_at = 2 * ROW_BYTES
+        active_at = {second: 3 * ROW_BYTES, third: 3 * ROW_BYTES + 4 * V}
+
         def activate(t):
-            if t in (pb, pc):
-                at = 6144 if t == pb else 7168
-                active_a[t] = staging.tile([P, V], F32, name="active_a%d" % t, align_bytes=64, offset=at)
+            if t in active_at:
+                active_a[t] = staging.tile([P, V], F32, name="active_a%d" % t, align_bytes=64, offset=active_at[t])
             else:
                 active_a[t] = sb.tile([P, V], F32, name="active_a%d" % t, align_bytes=64)
             nc.scalar.activation(active_a[t][:], picked_a[t][:], RELU)
 
-        activate(pa)
+        activate(first)
         w2_bf = sb.tile([P, N, PACK], BF16, name="w2_bf", align_bytes=64)
         nc.scalar.copy(
-            w2_bf[:].rearrange("p (c i) j -> p c j i", i=4),
-            w2_raw[:].rearrange("p j (c i) -> p c j i", i=4),
+            w2_bf[:].rearrange("p (c i) j -> p c j i", i=LINE),
+            w2_raw[:].rearrange("p j (c i) -> p c j i", i=LINE),
         )
-        activate(pb)
-        activate(pd)
+        activate(second)
+        activate(last)
 
         z_bf = [
-            staging.tile([P, HALF, PACK], BF16, name="z_bf%d" % h, align_bytes=64, offset=2048 * h) for h in range(2)
+            staging.tile([P, HALF, PACK], BF16, name="z_bf%d" % h, align_bytes=64, offset=z_bf_at[h]) for h in range(2)
         ]
         z = {}
 
         def put_b(t):
-            if t == pa:
+            if t == first:
                 z[t] = reused.tile([P, S], F32, name="z_first", align_bytes=64, offset=0)
-            elif t == pd:
-                z[t] = reused.tile([P, S], F32, name="z_last", align_bytes=64, offset=0)
-            elif t == pc:
-                z[t] = staging.tile([P, S], F32, name="z_third", align_bytes=64, offset=4096)
+            elif t == second:
+                z[t] = sb.tile([P, S], F32, name="z_second", tag="y%d" % last, align_bytes=64)
+            elif t == third:
+                z[t] = staging.tile([P, S], F32, name="z_third", align_bytes=64, offset=z_third_at)
             else:
-                z[t] = sb.tile([P, S], F32, name="z_second", tag="y%d" % pd, align_bytes=64)
-            nc.vector.tensor_tensor(z[t][:].indirect(lb_sb[:]), picked_b[t][:], gates[:, 1, :], MULT)
+                z[t] = reused.tile([P, S], F32, name="z_last", align_bytes=64, offset=0)
+            nc.vector.tensor_tensor(z[t][:].indirect(lb_sb[:]), picked_b[t][:], gate_b, MULT)
 
         def put_a(t):
-            nc.vector.tensor_tensor(z[t][:].indirect(la_sb[:]), active_a[t][:], gates[:, 0, :], MULT)
+            nc.vector.tensor_tensor(z[t][:].indirect(la_sb[:]), active_a[t][:], gate_a, MULT)
 
         def round_plane(t):
             nc.scalar.copy(z_bf[0][:, :, t], z[t][:, lo])
@@ -195,23 +209,25 @@ def tile_picked_tworoute_relu_p_kernel(
                 in_=w2_bf[:, half * N // 2 : (half + 1) * N // 2].rearrange("p c j -> p (c j)"),
             )
 
-        put_b(pa)
-        put_b(pb)
-        put_a(pa)
-        round_plane(pa)
-        activate(pc)
-        put_b(pc)
-        put_a(pb)
-        round_plane(pb)
-        put_b(pd)
-        put_a(pc)
-        round_plane(pc)
-        put_a(pd)
-        quantize_w2(0, staging.tile([P, N // 2], U32, name="w2_codes0", align_bytes=64, offset=7168))
-        q0, q1 = slice(0, P), slice(P, HALF)
-        for cols in (q0, q1):
-            nc.vector.tensor_copy(z_bf[0][:, cols, pd], z[pd][:, cols])
-        nc.scalar.copy(z_bf[1][:, :, pd], z[pd][:, hi])
+        put_b(first)
+        put_b(second)
+        put_a(first)
+        round_plane(first)
+        activate(third)
+        put_b(third)
+        put_a(second)
+        round_plane(second)
+        put_b(last)
+        put_a(third)
+        round_plane(third)
+        put_a(last)
+
+        quantize_w2(0, staging.tile([P, N // 2], U32, name="w2_codes0", align_bytes=64, offset=active_at[third]))
+        q0, q1, both = slice(0, P), slice(P, HALF), slice(0, HALF)
+        nc.vector.tensor_copy(z_bf[0][:, q0, last], z[last][:, q0])
+        nc.scalar.copy(z_bf[0][:, q1, last], z[last][:, q1])
+        nc.vector.tensor_copy(z_bf[1][:, :LAST_SPLIT, last], z[last][:, HALF : HALF + LAST_SPLIT])
+        nc.scalar.copy(z_bf[1][:, LAST_SPLIT:, last], z[last][:, HALF + LAST_SPLIT :])
 
         z_codes = [sb.tile([P, HALF], U32, name="z_codes%d" % h, align_bytes=64) for h in range(2)]
         z_scales = [sb.tile([P, HALF], U8, name="z_scales%d" % h, align_bytes=64) for h in range(2)]
@@ -225,14 +241,17 @@ def tile_picked_tworoute_relu_p_kernel(
 
         quantize_z(0, q0)
         quantize_z(0, q1)
-        quantize_z(1, lo)
+        quantize_z(1, both)
         quantize_w2(1, reused.tile([P, N // 2], U32, name="w2_codes1", align_bytes=64, offset=0))
 
+        steps = [(0, 0, q0), (1, 0, q0), (0, 0, q1), (1, 0, q1), (0, 1, both), (1, 1, both)]
+        steps.extend([(2, 0, both), (2, 1, both), (3, 0, both), (3, 1, q0), (3, 1, q1)])
+        scalar_alone = 4
         res = [sb.tile([P, S], F32, name="res%d" % r, align_bytes=64) for r in range(N // P)]
-        units = [(0, 0, q0), (0, 0, q1), (1, 0, lo), (0, 1, lo), (1, 1, lo), (2, 0, lo), (2, 1, lo), (3, 0, lo), (3, 1, q0), (3, 1, q1)]
-        for n, (r, h, cols) in enumerate(units):
+        for n, (r, h, cols) in enumerate(steps):
             w_cols = slice(r % 2 * P, (r % 2 + 1) * P)
-            acc = psum.tile([P, cols.stop - cols.start], F32, name="acc2", tag="bank%d" % ((6 + n) % 8))
+            bank = (banks_used + n) % BANKS
+            acc = psum.tile([P, cols.stop - cols.start], F32, name="acc2", tag="bank%d" % bank)
             nc.tensor.matmul_mx(
                 out=acc[:],
                 lhsT=w2_codes[r // 2][:, w_cols].bitcast(FP8X4),
@@ -243,11 +262,11 @@ def tile_picked_tworoute_relu_p_kernel(
                 stop=True,
             )
             tokens = slice(h * HALF + cols.start, h * HALF + cols.stop)
-            if n < 3 or n % 2 == 0:
+            if n < scalar_alone or (n - scalar_alone) % 2 == 1:
                 nc.scalar.copy(res[r][:, tokens], acc[:])
             else:
                 nc.vector.tensor_copy(res[r][:, tokens], acc[:])
-            if r < 2:
-                nc.sync.dma_start(out[r * P : (r + 1) * P, tokens], res[r][:, tokens])
-            elif tokens.stop == S:
-                nc.sync.dma_start(out[r * P : (r + 1) * P, :], res[r][:])
+            width = (tokens.stop - tokens.start, HALF, S, S)[r]
+            if tokens.stop % width == 0:
+                stored = slice(tokens.stop - width, tokens.stop)
+                nc.sync.dma_start(out[r * P : (r + 1) * P, stored], res[r][:, stored])

@@ -75,7 +75,7 @@ def tile_picked_tworoute_relu_p_kernel(
         nc.vector.tensor_copy(xs_picked[:], xs_all[:].indirect(offs_sb[:]))
         for q in range(4):
             rows = slice(scale_base + 4 * q, scale_base + 4 * q + 4)
-            nc.sync.dma_start(xs[32 * q : 32 * q + 4, :].bitcast(I32), xs_picked[rows, :].bitcast(I32))
+            nc.scalar.dma_start(xs[32 * q : 32 * q + 4, :].bitcast(I32), xs_picked[rows, :].bitcast(I32))
         nc.vector.tensor_copy(early_dst[:, first, :W1_SPLIT], early_src[:, first, :W1_SPLIT])
         nc.vector.tensor_copy(early_dst[:, second], early_src[:, second])
 

@@ -145,58 +145,60 @@ def tile_picked_tworoute_relu_p_kernel(
             nc.scalar.copy(y[t][:], acc[:])
         banks_used = len(pieces) + PACK - 1
 
-        picked_a, picked_b, active_a = {}, {}, {}
-        for t in PLANE_ORDER:
-            picked_b[t] = sb.tile([P, V], F32, name="picked_b", tag="picked_b%d" % t, align_bytes=64)
-            nc.vector.tensor_copy(picked_b[t][:], y[t][:].indirect(lb_sb[:]))
-            if t == first:
-                picked_a[t] = reused.tile([P, V], F32, name="picked_a_first", align_bytes=64, offset=0)
-            else:
-                picked_a[t] = sb.tile([P, V], F32, name="picked_a%d" % t, align_bytes=64)
-            nc.vector.tensor_copy(picked_a[t][:], y[t][:].indirect(la_sb[:]))
-
-        z_bf_at = (0, ROW_BYTES)
-        z_third_at = 2 * ROW_BYTES
-        active_at = {second: 3 * ROW_BYTES, third: 3 * ROW_BYTES + 4 * V}
-
-        def activate(t):
-            if t in active_at:
-                active_a[t] = staging.tile([P, V], F32, name="active_a%d" % t, align_bytes=64, offset=active_at[t])
-            else:
-                active_a[t] = sb.tile([P, V], F32, name="active_a%d" % t, align_bytes=64)
-            nc.scalar.activation(active_a[t][:], picked_a[t][:], RELU)
-
-        activate(first)
         w2_bf = sb.tile([P, N, PACK], BF16, name="w2_bf", align_bytes=64)
+        picked, active, z = {}, {}, {}
+        offsets = {"a": la_sb, "b": lb_sb}
+        gate = {"a": gate_a, "b": gate_b}
+
+        unit = 2 * V
+        picked_at = {
+            ("a", first): 3.5,
+            ("a", second): 5,
+            ("b", last): 4,
+            ("b", second): 10,
+            ("b", first): 12,
+            ("b", third): 14,
+            ("a", third): 16,
+            ("a", last): 14,
+        }
+        active_at = {first: 14, second: 16, third: 12, last: 18}
+        z_at = {second: 0, third: 6, first: 20, last: 24}
+        w2_codes0_at = 13
+
+        def fetch(route, t):
+            picked[route, t] = reused.tile(
+                [P, V], F32, name="picked_%s%d" % (route, t), align_bytes=64, offset=int(picked_at[route, t] * unit)
+            )
+            nc.vector.tensor_copy(picked[route, t][:], y[t][:].indirect(offsets[route][:]))
+            if route == "a":
+                active[t] = reused.tile([P, V], F32, name="active%d" % t, align_bytes=64, offset=active_at[t] * unit)
+                nc.scalar.activation(active[t][:], picked[route, t][:], RELU)
+
+        def put(route, t):
+            if route == "b":
+                z[t] = reused.tile([P, S], F32, name="z%d" % t, align_bytes=64, offset=z_at[t] * unit)
+            values = active[t] if route == "a" else picked[route, t]
+            nc.vector.tensor_tensor(z[t][:].indirect(offsets[route][:]), values[:], gate[route], MULT)
+            if route == "a" and t != last:
+                nc.scalar.copy(z_bf[0][:, :, t], z[t][:, lo])
+                nc.scalar.copy(z_bf[1][:, :, t], z[t][:, hi])
+
+        routes = [("b", first), ("a", first), ("b", second), ("a", second)]
+        routes.extend([("b", third), ("b", last), ("a", third), ("a", last)])
+        fetch(*routes[0])
+        fetch(*routes[1])
         nc.scalar.copy(
             w2_bf[:].rearrange("p (c i) j -> p c j i", i=LINE),
             w2_raw[:].rearrange("p j (c i) -> p c j i", i=LINE),
         )
-        activate(second)
-        activate(last)
-
         z_bf = [
-            staging.tile([P, HALF, PACK], BF16, name="z_bf%d" % h, align_bytes=64, offset=z_bf_at[h]) for h in range(2)
+            staging.tile([P, HALF, PACK], BF16, name="z_bf%d" % h, align_bytes=64, offset=h * ROW_BYTES)
+            for h in range(2)
         ]
-        z = {}
-
-        def put_b(t):
-            if t == first:
-                z[t] = reused.tile([P, S], F32, name="z_first", align_bytes=64, offset=0)
-            elif t == second:
-                z[t] = sb.tile([P, S], F32, name="z_second", tag="y%d" % last, align_bytes=64)
-            elif t == third:
-                z[t] = staging.tile([P, S], F32, name="z_third", align_bytes=64, offset=z_third_at)
-            else:
-                z[t] = reused.tile([P, S], F32, name="z_last", align_bytes=64, offset=0)
-            nc.vector.tensor_tensor(z[t][:].indirect(lb_sb[:]), picked_b[t][:], gate_b, MULT)
-
-        def put_a(t):
-            nc.vector.tensor_tensor(z[t][:].indirect(la_sb[:]), active_a[t][:], gate_a, MULT)
-
-        def round_plane(t):
-            nc.scalar.copy(z_bf[0][:, :, t], z[t][:, lo])
-            nc.scalar.copy(z_bf[1][:, :, t], z[t][:, hi])
+        for n, route in enumerate(routes):
+            put(*route)
+            if n + 2 < len(routes):
+                fetch(*routes[n + 2])
 
         w2_codes, w2_scales = [], []
 
@@ -209,20 +211,7 @@ def tile_picked_tworoute_relu_p_kernel(
                 in_=w2_bf[:, half * N // 2 : (half + 1) * N // 2].rearrange("p c j -> p (c j)"),
             )
 
-        put_b(first)
-        put_b(second)
-        put_a(first)
-        round_plane(first)
-        activate(third)
-        put_b(third)
-        put_a(second)
-        round_plane(second)
-        put_b(last)
-        put_a(third)
-        round_plane(third)
-        put_a(last)
-
-        quantize_w2(0, staging.tile([P, N // 2], U32, name="w2_codes0", align_bytes=64, offset=active_at[third]))
+        quantize_w2(0, reused.tile([P, N // 2], U32, name="w2_codes0", align_bytes=64, offset=w2_codes0_at * unit))
         q0, q1, both = slice(0, P), slice(P, HALF), slice(0, HALF)
         nc.vector.tensor_copy(z_bf[0][:, q0, last], z[last][:, q0])
         nc.scalar.copy(z_bf[0][:, q1, last], z[last][:, q1])
@@ -242,7 +231,7 @@ def tile_picked_tworoute_relu_p_kernel(
         quantize_z(0, q0)
         quantize_z(0, q1)
         quantize_z(1, both)
-        quantize_w2(1, reused.tile([P, N // 2], U32, name="w2_codes1", align_bytes=64, offset=0))
+        quantize_w2(1, reused.tile([P, N // 2], U32, name="w2_codes1", align_bytes=64, offset=z_at[last] * unit))
 
         steps = [(0, 0, q0), (1, 0, q0), (0, 0, q1), (1, 0, q1), (0, 1, both), (1, 1, both)]
         steps.extend([(2, 0, both), (2, 1, both), (3, 0, both), (3, 1, q0), (3, 1, q1)])

@@ -145,7 +145,7 @@ def tile_picked_tworoute_relu_p_kernel(
             nc.scalar.copy(y[t][:], acc[:])
         banks_used = len(pieces) + PACK - 1
 
-        w2_bf = sb.tile([P, N, PACK], BF16, name="w2_bf", align_bytes=64)
+        w2_bf = sb.tile([P, N - P, PACK], BF16, name="w2_bf", align_bytes=64)
         picked, active, z = {}, {}, {}
         offsets = {"a": la_sb, "b": lb_sb}
         gate = {"a": gate_a, "b": gate_b}
@@ -163,7 +163,6 @@ def tile_picked_tworoute_relu_p_kernel(
         }
         active_at = {first: 14, second: 16, third: 12, last: 18}
         z_at = {second: 0, third: 6, first: 20, last: 24}
-        w2_codes0_at = 13
 
         def fetch(route, t):
             picked[route, t] = reused.tile(
@@ -187,31 +186,34 @@ def tile_picked_tworoute_relu_p_kernel(
         routes.extend([("b", third), ("b", last), ("a", third), ("a", last)])
         fetch(*routes[0])
         fetch(*routes[1])
-        nc.scalar.copy(
-            w2_bf[:].rearrange("p (c i) j -> p c j i", i=LINE),
-            w2_raw[:].rearrange("p j (c i) -> p c j i", i=LINE),
-        )
-        z_bf = [
-            staging.tile([P, HALF, PACK], BF16, name="z_bf%d" % h, align_bytes=64, offset=h * ROW_BYTES)
-            for h in range(2)
-        ]
+        def lay_out_w2(laid, cols):
+            nc.scalar.copy(
+                laid.rearrange("p (c i) j -> p c j i", i=LINE),
+                w2_raw[:, :, cols].rearrange("p j (c i) -> p c j i", i=LINE),
+            )
+
+        lay_out_w2(w2_bf[:], slice(P, N))
+        z_bf = [sb.tile([P, HALF, PACK], BF16, name="z_bf%d" % h, align_bytes=64) for h in range(2)]
         for n, route in enumerate(routes):
             put(*route)
             if n + 2 < len(routes):
                 fetch(*routes[n + 2])
+            if n + 3 == len(routes):
+                at = picked_at["a", last] * unit
+                w2_bf0 = reused.tile([P, P, PACK], BF16, name="w2_bf0", align_bytes=64, offset=at)
+                lay_out_w2(w2_bf0[:], slice(0, P))
 
         w2_codes, w2_scales = [], []
 
-        def quantize_w2(half, codes):
-            w2_codes.append(codes)
-            w2_scales.append(sb.tile([P, N // 2], U8, name="w2_scales%d" % half, align_bytes=64))
-            nc.vector.quantize_mx(
-                out=w2_codes[half][:].bitcast(FP8X4),
-                scales=w2_scales[half][:],
-                in_=w2_bf[:, half * N // 2 : (half + 1) * N // 2].rearrange("p c j -> p (c j)"),
-            )
+        def quantize_w2(laid, codes):
+            scales = sb.tile([P, laid.shape[1]], U8, name="w2_scales%d" % len(w2_codes), align_bytes=64)
+            nc.vector.quantize_mx(out=codes[:].bitcast(FP8X4), scales=scales[:], in_=laid.rearrange("p c j -> p (c j)"))
+            for r in range(laid.shape[1] // P):
+                w2_codes.append(codes[:, r * P : (r + 1) * P])
+                w2_scales.append(scales[:, r * P : (r + 1) * P])
 
-        quantize_w2(0, reused.tile([P, N // 2], U32, name="w2_codes0", align_bytes=64, offset=w2_codes0_at * unit))
+        quantize_w2(w2_bf0[:], sb.tile([P, P], U32, name="w2_codes0", align_bytes=64))
+        quantize_w2(w2_bf[:, :P], reused.tile([P, P], U32, name="w2_codes1", align_bytes=64, offset=at))
         q0, q1, both = slice(0, P), slice(P, HALF), slice(0, HALF)
         nc.vector.tensor_copy(z_bf[0][:, q0, last], z[last][:, q0])
         nc.scalar.copy(z_bf[0][:, q1, last], z[last][:, q1])
@@ -231,20 +233,19 @@ def tile_picked_tworoute_relu_p_kernel(
         quantize_z(0, q0)
         quantize_z(0, q1)
         quantize_z(1, both)
-        quantize_w2(1, reused.tile([P, N // 2], U32, name="w2_codes1", align_bytes=64, offset=z_at[last] * unit))
+        quantize_w2(w2_bf[:, P:], reused.tile([P, N // 2], U32, name="w2_codes2", align_bytes=64, offset=z_at[last] * unit))
 
         steps = [(0, 0, q0), (1, 0, q0), (0, 0, q1), (1, 0, q1), (0, 1, both), (1, 1, both)]
         steps.extend([(2, 0, both), (2, 1, both), (3, 0, both), (3, 1, q0), (3, 1, q1)])
         scalar_alone = 4
         res = [sb.tile([P, S], F32, name="res%d" % r, align_bytes=64) for r in range(N // P)]
         for n, (r, h, cols) in enumerate(steps):
-            w_cols = slice(r % 2 * P, (r % 2 + 1) * P)
             bank = (banks_used + n) % BANKS
             acc = psum.tile([P, cols.stop - cols.start], F32, name="acc2", tag="bank%d" % bank)
             nc.tensor.matmul_mx(
                 out=acc[:],
-                lhsT=w2_codes[r // 2][:, w_cols].bitcast(FP8X4),
-                lhsT_scale=w2_scales[r // 2][:, w_cols],
+                lhsT=w2_codes[r].bitcast(FP8X4),
+                lhsT_scale=w2_scales[r],
                 rhs=z_codes[h][:, cols].bitcast(FP8X4),
                 rhs_scale=z_scales[h][:, cols],
                 start=True,

@@ -28,6 +28,7 @@ ROW_BYTES = 4 * H
 W1_SPLIT = 10
 LAST_SPLIT = 160
 PLANE_ORDER = (0, 2, 3, 1)
+W2_LATE = 64
 
 
 def tile_picked_tworoute_relu_p_kernel(
@@ -145,7 +146,7 @@ def tile_picked_tworoute_relu_p_kernel(
             nc.scalar.copy(y[t][:], acc[:])
         banks_used = len(pieces) + PACK - 1
 
-        w2_bf = sb.tile([P, N - P, PACK], BF16, name="w2_bf", align_bytes=64)
+        w2_bf = sb.tile([P, N - W2_LATE, PACK], BF16, name="w2_bf", align_bytes=64)
         picked, active, z = {}, {}, {}
         offsets = {"a": la_sb, "b": lb_sb}
         gate = {"a": gate_a, "b": gate_b}
@@ -192,7 +193,7 @@ def tile_picked_tworoute_relu_p_kernel(
                 w2_raw[:, :, cols].rearrange("p j (c i) -> p c j i", i=LINE),
             )
 
-        lay_out_w2(w2_bf[:], slice(P, N))
+        lay_out_w2(w2_bf[:], slice(0, N - W2_LATE))
         z_bf = [sb.tile([P, HALF, PACK], BF16, name="z_bf%d" % h, align_bytes=64) for h in range(2)]
         for n, route in enumerate(routes):
             put(*route)
@@ -200,20 +201,18 @@ def tile_picked_tworoute_relu_p_kernel(
                 fetch(*routes[n + 2])
             if n + 3 == len(routes):
                 at = picked_at["a", last] * unit
-                w2_bf0 = reused.tile([P, P, PACK], BF16, name="w2_bf0", align_bytes=64, offset=at)
-                lay_out_w2(w2_bf0[:], slice(0, P))
+                w2_bf3 = reused.tile([P, W2_LATE, PACK], BF16, name="w2_bf3", align_bytes=64, offset=at)
+                lay_out_w2(w2_bf3[:], slice(N - W2_LATE, N))
 
-        w2_codes, w2_scales = [], []
+        w2_scales = sb.tile([P, N], U8, name="w2_scales", align_bytes=64)
 
-        def quantize_w2(laid, codes):
-            scales = sb.tile([P, laid.shape[1]], U8, name="w2_scales%d" % len(w2_codes), align_bytes=64)
-            nc.vector.quantize_mx(out=codes[:].bitcast(FP8X4), scales=scales[:], in_=laid.rearrange("p c j -> p (c j)"))
-            for r in range(laid.shape[1] // P):
-                w2_codes.append(codes[:, r * P : (r + 1) * P])
-                w2_scales.append(scales[:, r * P : (r + 1) * P])
+        def quantize_w2(laid, codes, cols):
+            nc.vector.quantize_mx(
+                out=codes.bitcast(FP8X4), scales=w2_scales[:, cols], in_=laid.rearrange("p c j -> p (c j)")
+            )
 
-        quantize_w2(w2_bf0[:], sb.tile([P, P], U32, name="w2_codes0", align_bytes=64))
-        quantize_w2(w2_bf[:, :P], reused.tile([P, P], U32, name="w2_codes1", align_bytes=64, offset=at))
+        w2_lower = staging.tile([P, N // 2], U32, name="w2_lower", align_bytes=64, offset=0)
+        quantize_w2(w2_bf[:, : N // 2], w2_lower[:], slice(0, N // 2))
         q0, q1, both = slice(0, P), slice(P, HALF), slice(0, HALF)
         nc.vector.tensor_copy(z_bf[0][:, q0, last], z[last][:, q0])
         nc.scalar.copy(z_bf[0][:, q1, last], z[last][:, q1])
@@ -233,19 +232,26 @@ def tile_picked_tworoute_relu_p_kernel(
         quantize_z(0, q0)
         quantize_z(0, q1)
         quantize_z(1, both)
-        quantize_w2(w2_bf[:, P:], reused.tile([P, N // 2], U32, name="w2_codes2", align_bytes=64, offset=z_at[last] * unit))
+        w2_upper = reused.tile([P, N // 2], U32, name="w2_upper", align_bytes=64, offset=z_at[last] * unit)
+        early_end = N - W2_LATE
+        quantize_w2(w2_bf[:, 2 * P : 3 * P], w2_upper[:, :P], slice(2 * P, 3 * P))
+        quantize_w2(w2_bf[:, 3 * P :], w2_upper[:, P : early_end - N // 2], slice(3 * P, early_end))
+        quantize_w2(w2_bf3[:], w2_upper[:, early_end - N // 2 :], slice(early_end, N))
+        w2_codes = [w2_lower[:, :P], w2_lower[:, P:], w2_upper[:, :P], w2_upper[:, P:]]
 
         steps = [(0, 0, q0), (1, 0, q0), (0, 0, q1), (1, 0, q1), (0, 1, both), (1, 1, both)]
         steps.extend([(2, 0, both), (2, 1, both), (3, 0, both), (3, 1, q0), (3, 1, q1)])
         scalar_alone = 4
+        banks = [(banks_used + n) % BANKS for n in range(len(steps))]
+        banks[7], banks[8] = banks[8], banks[7]
         res = [sb.tile([P, S], F32, name="res%d" % r, align_bytes=64) for r in range(N // P)]
         for n, (r, h, cols) in enumerate(steps):
-            bank = (banks_used + n) % BANKS
+            bank = banks[n]
             acc = psum.tile([P, cols.stop - cols.start], F32, name="acc2", tag="bank%d" % bank)
             nc.tensor.matmul_mx(
                 out=acc[:],
                 lhsT=w2_codes[r].bitcast(FP8X4),
-                lhsT_scale=w2_scales[r],
+                lhsT_scale=w2_scales[:, r * P : (r + 1) * P],
                 rhs=z_codes[h][:, cols].bitcast(FP8X4),
                 rhs_scale=z_scales[h][:, cols],
                 start=True,

@@ -15,6 +15,7 @@ U8 = mybir.dt.uint8
 FP8X4 = mybir.dt.float8_e4m3fn_x4
 MULT = mybir.AluOpType.mult
 RELU = mybir.ActivationFunctionType.Relu
+COPY = mybir.ActivationFunctionType.Copy
 
 P = 128
 PACK = 4
@@ -26,7 +27,7 @@ BANKS = 8
 HALF = S // 2
 ROW_BYTES = 4 * H
 W1_SPLIT = 10
-LAST_SPLIT = 160
+LAST_SPLIT = 128
 PLANE_ORDER = (0, 2, 3, 1)
 W2_LATE = 64
 
@@ -129,7 +130,7 @@ def tile_picked_tworoute_relu_p_kernel(
             )
             return acc
 
-        lo, hi = slice(0, HALF), slice(HALF, S)
+        lo = slice(0, HALF)
         y = {}
         for t in PLANE_ORDER:
             y[t] = sb.tile([P, S], F32, name="y", tag="y%d" % t, align_bytes=64)
@@ -141,83 +142,95 @@ def tile_picked_tworoute_relu_p_kernel(
         for bank, (cols, copy_out) in enumerate(pieces):
             acc = first_product(first, cols, bank)
             copy_out(y[first][:, cols], acc[:])
-        for bank, t in enumerate(PLANE_ORDER[1:], len(pieces)):
-            acc = first_product(t, slice(0, S), bank)
-            nc.scalar.copy(y[t][:], acc[:])
-        banks_used = len(pieces) + PACK - 1
 
-        w2_bf = sb.tile([P, N - W2_LATE, PACK], BF16, name="w2_bf", align_bytes=64)
-        picked, active, z = {}, {}, {}
-        offsets = {"a": la_sb, "b": lb_sb}
-        gate = {"a": gate_a, "b": gate_b}
+        w2_bf = sb.tile([P, N, PACK], BF16, name="w2_bf", align_bytes=64)
 
-        unit = 2 * V
-        picked_at = {
-            ("a", first): 3.5,
-            ("a", second): 5,
-            ("b", last): 4,
-            ("b", second): 10,
-            ("b", first): 12,
-            ("b", third): 14,
-            ("a", third): 16,
-            ("a", last): 14,
-        }
-        active_at = {first: 14, second: 16, third: 12, last: 18}
-        z_at = {second: 0, third: 6, first: 20, last: 24}
-
-        def fetch(route, t):
-            picked[route, t] = reused.tile(
-                [P, V], F32, name="picked_%s%d" % (route, t), align_bytes=64, offset=int(picked_at[route, t] * unit)
-            )
-            nc.vector.tensor_copy(picked[route, t][:], y[t][:].indirect(offsets[route][:]))
-            if route == "a":
-                active[t] = reused.tile([P, V], F32, name="active%d" % t, align_bytes=64, offset=active_at[t] * unit)
-                nc.scalar.activation(active[t][:], picked[route, t][:], RELU)
-
-        def put(route, t):
-            if route == "b":
-                z[t] = reused.tile([P, S], F32, name="z%d" % t, align_bytes=64, offset=z_at[t] * unit)
-            values = active[t] if route == "a" else picked[route, t]
-            nc.vector.tensor_tensor(z[t][:].indirect(offsets[route][:]), values[:], gate[route], MULT)
-            if route == "a" and t != last:
-                nc.scalar.copy(z_bf[0][:, :, t], z[t][:, lo])
-                nc.scalar.copy(z_bf[1][:, :, t], z[t][:, hi])
-
-        routes = [("b", first), ("a", first), ("b", second), ("a", second)]
-        routes.extend([("b", third), ("b", last), ("a", third), ("a", last)])
-        fetch(*routes[0])
-        fetch(*routes[1])
-        def lay_out_w2(laid, cols):
+        def lay_out_w2(cols):
             nc.scalar.copy(
-                laid.rearrange("p (c i) j -> p c j i", i=LINE),
+                w2_bf[:, cols].rearrange("p (c i) j -> p c j i", i=LINE),
                 w2_raw[:, :, cols].rearrange("p j (c i) -> p c j i", i=LINE),
             )
 
-        lay_out_w2(w2_bf[:], slice(0, N - W2_LATE))
+        picked, z = {}, {}
+        offsets = {"a": la_sb, "b": lb_sb}
+        gate = {"a": gate_a, "b": gate_b}
         z_bf = [sb.tile([P, HALF, PACK], BF16, name="z_bf%d" % h, align_bytes=64) for h in range(2)]
-        for n, route in enumerate(routes):
-            put(*route)
-            if n + 2 < len(routes):
-                fetch(*routes[n + 2])
-            if n + 3 == len(routes):
-                at = picked_at["a", last] * unit
-                w2_bf3 = reused.tile([P, W2_LATE, PACK], BF16, name="w2_bf3", align_bytes=64, offset=at)
-                lay_out_w2(w2_bf3[:], slice(N - W2_LATE, N))
+        for t in PLANE_ORDER:
+            z[t] = reused.tile([P, S], F32, name="z%d" % t, align_bytes=64, offset=t * 4 * S)
+
+        def empty_plane(t, bank):
+            acc = first_product(t, slice(0, S), bank)
+            nc.scalar.copy(y[t][:], acc[:])
+
+        def fetch(route, t):
+            picked[route, t] = sb.tile([P, V], F32, name="picked_%s%d" % (route, t), align_bytes=64)
+            window = y[t][:].indirect(offsets[route][:])
+            if (route, t) == ("b", first):
+                nc.vector.tensor_copy(picked[route, t][:], window)
+            else:
+                nc.scalar.activation(picked[route, t][:], window, COPY)
+
+        def activate(t):
+            active = sb.tile([P, V], F32, name="active%d" % t, align_bytes=64)
+            nc.scalar.activation(active[:], picked["a", t][:], RELU)
+            picked["a", t] = active
+
+        def put(route, t):
+            nc.vector.tensor_tensor(z[t][:].indirect(offsets[route][:]), picked[route, t][:], gate[route], MULT)
+
+        def round_plane(copy, t, h, cols):
+            copy(z_bf[h][:, cols, t], z[t][:, h * HALF + cols.start : h * HALF + cols.stop])
+
+        q0, q1, both = slice(0, P), slice(P, HALF), slice(0, HALF)
+        fetch("b", first)
+        put("b", first)
+        empty_plane(second, 3)
+        fetch("b", second)
+        put("b", second)
+        fetch("a", first)
+        fetch("a", second)
+        activate(first)
+        put("a", first)
+        activate(second)
+        put("a", second)
+        empty_plane(third, 4)
+        fetch("b", third)
+        put("b", third)
+        empty_plane(last, 5)
+        fetch("b", last)
+        put("b", last)
+        banks_used = 6
+        lay_out_w2(slice(0, 2 * P - W2_LATE))
+        for h in range(2):
+            round_plane(nc.scalar.copy, first, h, both)
+        fetch("a", third)
+        lay_out_w2(slice(2 * P, 3 * P))
+        activate(third)
+        put("a", third)
+        round_plane(nc.scalar.copy, second, 0, both)
+        fetch("a", last)
+        round_plane(nc.scalar.copy, second, 1, both)
+        activate(last)
+        put("a", last)
+        lay_out_w2(slice(2 * P - W2_LATE, 2 * P))
 
         w2_scales = sb.tile([P, N], U8, name="w2_scales", align_bytes=64)
 
-        def quantize_w2(laid, codes, cols):
+        def quantize_w2(codes, cols):
             nc.vector.quantize_mx(
-                out=codes.bitcast(FP8X4), scales=w2_scales[:, cols], in_=laid.rearrange("p c j -> p (c j)")
+                out=codes.bitcast(FP8X4), scales=w2_scales[:, cols], in_=w2_bf[:, cols].rearrange("p c j -> p (c j)")
             )
 
-        w2_lower = staging.tile([P, N // 2], U32, name="w2_lower", align_bytes=64, offset=0)
-        quantize_w2(w2_bf[:, : N // 2], w2_lower[:], slice(0, N // 2))
-        q0, q1, both = slice(0, P), slice(P, HALF), slice(0, HALF)
-        nc.vector.tensor_copy(z_bf[0][:, q0, last], z[last][:, q0])
-        nc.scalar.copy(z_bf[0][:, q1, last], z[last][:, q1])
-        nc.vector.tensor_copy(z_bf[1][:, :LAST_SPLIT, last], z[last][:, HALF : HALF + LAST_SPLIT])
-        nc.scalar.copy(z_bf[1][:, LAST_SPLIT:, last], z[last][:, HALF + LAST_SPLIT :])
+        w2_lower = sb.tile([P, N // 2], U32, name="w2_lower", align_bytes=64)
+        quantize_w2(w2_lower[:], slice(0, N // 2))
+        round_plane(nc.scalar.copy, third, 0, q0)
+        round_plane(nc.scalar.copy, third, 0, q1)
+        round_plane(nc.scalar.copy, third, 1, both)
+        round_plane(nc.vector.tensor_copy, last, 0, q0)
+        round_plane(nc.vector.tensor_copy, last, 0, q1)
+        round_plane(nc.vector.tensor_copy, last, 1, slice(0, LAST_SPLIT))
+        round_plane(nc.scalar.copy, last, 1, slice(LAST_SPLIT, HALF))
+        lay_out_w2(slice(3 * P, N))
 
         z_codes = [sb.tile([P, HALF], U32, name="z_codes%d" % h, align_bytes=64) for h in range(2)]
         z_scales = [sb.tile([P, HALF], U8, name="z_scales%d" % h, align_bytes=64) for h in range(2)]
@@ -232,11 +245,9 @@ def tile_picked_tworoute_relu_p_kernel(
         quantize_z(0, q0)
         quantize_z(0, q1)
         quantize_z(1, both)
-        w2_upper = reused.tile([P, N // 2], U32, name="w2_upper", align_bytes=64, offset=z_at[last] * unit)
-        early_end = N - W2_LATE
-        quantize_w2(w2_bf[:, 2 * P : 3 * P], w2_upper[:, :P], slice(2 * P, 3 * P))
-        quantize_w2(w2_bf[:, 3 * P :], w2_upper[:, P : early_end - N // 2], slice(3 * P, early_end))
-        quantize_w2(w2_bf3[:], w2_upper[:, early_end - N // 2 :], slice(early_end, N))
+        w2_upper = reused.tile([P, N // 2], U32, name="w2_upper", align_bytes=64, offset=last * 4 * S)
+        quantize_w2(w2_upper[:, :P], slice(2 * P, 3 * P))
+        quantize_w2(w2_upper[:, P:], slice(3 * P, N))
         w2_codes = [w2_lower[:, :P], w2_lower[:, P:], w2_upper[:, :P], w2_upper[:, P:]]
 
         steps = [(0, 0, q0), (1, 0, q0), (0, 0, q1), (1, 0, q1), (0, 1, both), (1, 1, both)]

@@ -58,7 +58,7 @@ def tile_picked_tworoute_relu_p_kernel(
         nc.sync.dma_start(w1_early[:], w1_rows[:, :1])
         nc.sync.dma_start(offs_sb[:], offs)
         nc.sync.dma_start(xs_all[scale_base:, :].bitcast(I32), x_scales[0].bitcast(I32))
-        xw_all = sb.tile([P, T], I32, name="xw_all", align_bytes=64)
+        xw_all = sb.tile([P, T], I32, name="xw_all", tag="stage_x", align_bytes=64)
         nc.sync.dma_start(xw_all[:], x_words[0].rearrange("p n t -> p (n t)").bitcast(I32))
         w1_late = staging.tile([P, PACK - 1, H], F32, name="w1_late", align_bytes=64, offset=ROW_BYTES)
         nc.sync.dma_start(w1_late[:], w1_rows[:, 1:])
@@ -112,7 +112,7 @@ def tile_picked_tworoute_relu_p_kernel(
         gate_a, gate_b = gates[:, 0, :], gates[:, 1, :]
         nc.sync.dma_start(gate_b, wb.rearrange("(b t r) v -> t b r v", t=PACK, r=RUN)[0])
         nc.sync.dma_start(gate_a, wa.rearrange("(b t r) v -> t b r v", t=PACK, r=RUN)[0])
-        w2_raw = staging.tile([P, PACK, N], F32, name="w2_raw", align_bytes=64, offset=0)
+        w2_raw = sb.tile([P, PACK, N], F32, name="w2_raw", tag="stage_x", align_bytes=64)
         w2_rows = w2.rearrange("(b t r) c -> t b r c", t=PACK, r=RUN)
         for t in range(PACK):
             nc.sync.dma_start(w2_raw[:, t, :], w2_rows[t])
@@ -156,7 +156,8 @@ def tile_picked_tworoute_relu_p_kernel(
         gate = {"a": gate_a, "b": gate_b}
         z_bf = [sb.tile([P, HALF, PACK], BF16, name="z_bf%d" % h, align_bytes=64) for h in range(2)]
         for t in PLANE_ORDER:
-            z[t] = reused.tile([P, S], F32, name="z%d" % t, align_bytes=64, offset=t * 4 * S)
+            width = 2 * S if t == first else S
+            z[t] = reused.tile([P, width], F32, name="z%d" % t, align_bytes=64, offset=t * 8 * S)
 
         def empty_plane(t, bank):
             acc = first_product(t, slice(0, S), bank)
@@ -201,15 +202,16 @@ def tile_picked_tworoute_relu_p_kernel(
         put("b", last)
         banks_used = 6
         lay_out_w2(slice(0, 2 * P - W2_LATE))
-        for h in range(2):
-            round_plane(nc.scalar.copy, first, h, both)
         fetch("a", third)
         lay_out_w2(slice(2 * P, 3 * P))
         activate(third)
         put("a", third)
-        round_plane(nc.scalar.copy, second, 0, both)
+        nc.scalar.copy(z[first][:, S:], z[second][:])
         fetch("a", last)
-        round_plane(nc.scalar.copy, second, 1, both)
+        pair = z[first][:].rearrange("p (t c) -> p c t", t=2)
+        for h in range(2):
+            nc.scalar.copy(z_bf[h][:, :, first : second + 1 : second - first], pair[:, h * HALF : (h + 1) * HALF])
+        lay_out_w2(slice(3 * P, N))
         activate(last)
         put("a", last)
         lay_out_w2(slice(2 * P - W2_LATE, 2 * P))
@@ -230,7 +232,6 @@ def tile_picked_tworoute_relu_p_kernel(
         round_plane(nc.vector.tensor_copy, last, 0, q1)
         round_plane(nc.vector.tensor_copy, last, 1, slice(0, LAST_SPLIT))
         round_plane(nc.scalar.copy, last, 1, slice(LAST_SPLIT, HALF))
-        lay_out_w2(slice(3 * P, N))
 
         z_codes = [sb.tile([P, HALF], U32, name="z_codes%d" % h, align_bytes=64) for h in range(2)]
         z_scales = [sb.tile([P, HALF], U8, name="z_scales%d" % h, align_bytes=64) for h in range(2)]
@@ -245,7 +246,7 @@ def tile_picked_tworoute_relu_p_kernel(
         quantize_z(0, q0)
         quantize_z(0, q1)
         quantize_z(1, both)
-        w2_upper = reused.tile([P, N // 2], U32, name="w2_upper", align_bytes=64, offset=last * 4 * S)
+        w2_upper = reused.tile([P, N // 2], U32, name="w2_upper", align_bytes=64, offset=last * 8 * S)
         quantize_w2(w2_upper[:, :P], slice(2 * P, 3 * P))
         quantize_w2(w2_upper[:, P:], slice(3 * P, N))
         w2_codes = [w2_lower[:, :P], w2_lower[:, P:], w2_upper[:, :P], w2_upper[:, P:]]

@@ -135,8 +135,8 @@ def tile_picked_tworoute_relu_p_kernel(
         for t in PLANE_ORDER:
             y[t] = sb.tile([P, S], F32, name="y", tag="y%d" % t, align_bytes=64)
         pieces = (
-            (lo, nc.scalar.copy),
-            (slice(HALF, HALF + P), nc.vector.tensor_copy),
+            (lo, nc.vector.tensor_copy),
+            (slice(HALF, HALF + P), nc.scalar.copy),
             (slice(HALF + P, S), nc.scalar.copy),
         )
         for bank, (cols, copy_out) in enumerate(pieces):
@@ -159,15 +159,17 @@ def tile_picked_tworoute_relu_p_kernel(
             width = 2 * S if t == first else S
             z[t] = reused.tile([P, width], F32, name="z%d" % t, align_bytes=64, offset=t * 8 * S)
 
-        def empty_plane(t, bank):
-            acc = first_product(t, slice(0, S), bank)
-            nc.scalar.copy(y[t][:], acc[:])
+        def empty_plane(t, bank, cols):
+            acc = first_product(t, cols, bank)
+            nc.scalar.copy(y[t][:, cols], acc[:])
 
         def fetch(route, t):
             picked[route, t] = sb.tile([P, V], F32, name="picked_%s%d" % (route, t), align_bytes=64)
             window = y[t][:].indirect(offsets[route][:])
             if (route, t) == ("b", first):
-                nc.vector.tensor_copy(picked[route, t][:], window)
+                cut = V // 2 // LIST_ROWS
+                nc.vector.tensor_copy(picked[route, t][:, : V // 2], y[t][:].indirect(lb_sb[:, :cut]))
+                nc.scalar.activation(picked[route, t][:, V // 2 :], y[t][:].indirect(lb_sb[:, cut:]), COPY)
             else:
                 nc.scalar.activation(picked[route, t][:], window, COPY)
 
@@ -185,7 +187,10 @@ def tile_picked_tworoute_relu_p_kernel(
         q0, q1, both = slice(0, P), slice(P, HALF), slice(0, HALF)
         fetch("b", first)
         put("b", first)
-        empty_plane(second, 3)
+        empty_plane(second, 3, slice(0, P))
+        empty_plane(second, 4, slice(P, HALF))
+        empty_plane(second, 5, slice(HALF, S))
+        empty_plane(third, 6, slice(0, HALF))
         fetch("b", second)
         put("b", second)
         fetch("a", first)
@@ -194,13 +199,13 @@ def tile_picked_tworoute_relu_p_kernel(
         put("a", first)
         activate(second)
         put("a", second)
-        empty_plane(third, 4)
+        empty_plane(third, 7, slice(HALF, S))
         fetch("b", third)
         put("b", third)
-        empty_plane(last, 5)
+        empty_plane(last, 0, slice(0, S))
         fetch("b", last)
         put("b", last)
-        banks_used = 6
+        banks_used = 1
         lay_out_w2(slice(0, 2 * P - W2_LATE))
         fetch("a", third)
         lay_out_w2(slice(2 * P, 3 * P))

from contextlib import ExitStack

import concourse.mybir as mybir

K, T, S, V, N, H = 512, 2048, 512, 256, 512, 512
FLOPS = 2 * K * H * S + 2 * H * N * S
BYTES = K * T + 16 * T + 4 * K * H + 4 * H * N + 2 * 4 * 8 * V + 2 * 128 * (S + 2 * V) // 16 + 4 * N * S

F32 = mybir.dt.float32
BF16 = mybir.dt.bfloat16
I32 = mybir.dt.int32
U32 = mybir.dt.uint32
U16 = mybir.dt.uint16
U8 = mybir.dt.uint8
FP8X4 = mybir.dt.float8_e4m3fn_x4
MULT = mybir.AluOpType.mult
RELU = mybir.ActivationFunctionType.Relu
COPY = mybir.ActivationFunctionType.Copy

P = 128
PACK = 4
RUN = 8
LIST_ROWS = 16
SCALE_ROWS = K // 32
LINE = 4
BANKS = 8
HALF = S // 2
ROW_BYTES = 4 * H
W1_SPLIT = 10
LAST_SPLIT = 128
PLANE_ORDER = (0, 2, 3, 1)
W2_LATE = 64


def tile_picked_tworoute_relu_p_kernel(
    tc, x_words, x_scales, w1, wa, wb, w2, offs, la, lb, out
):
    nc = tc.nc
    with ExitStack() as ctx:
        lists = ctx.enter_context(tc.tile_pool(name="lists", bufs=1))
        sb = ctx.enter_context(tc.tile_pool(name="sb", bufs=1))
        reused = ctx.enter_context(tc.tile_pool(name="reused", bufs=1))
        staging = ctx.enter_context(tc.tile_pool(name="staging", bufs=1))
        psum = ctx.enter_context(tc.psum_pool(name="psum", bufs=1))

        offs_sb = lists.tile([P, S // LIST_ROWS], U16, name="offs_sb")
        la_sb = lists.tile([P, V // LIST_ROWS], U16, name="la_sb")
        lb_sb = lists.tile([P, V // LIST_ROWS], U16, name="lb_sb")

        scale_base = P - SCALE_ROWS
        xs_all = sb.tile([P, T], U8, name="xs_all", tag="stage_c", align_bytes=64)
        nc.vector.memset(xs_all[:scale_base, :].bitcast(I32), 0)
        xs = sb.tile([P, S], U8, name="xs", align_bytes=64)
        nc.vector.memset(xs[:].bitcast(I32), 0)

        w1_rows = w1.rearrange("(p j) c -> p j c", j=PACK)
        w1_early = staging.tile([P, 1, H], F32, name="w1_early", align_bytes=64, offset=0)
        nc.sync.dma_start(w1_early[:], w1_rows[:, :1])
        nc.sync.dma_start(offs_sb[:], offs)
        nc.sync.dma_start(xs_all[scale_base:, :].bitcast(I32), x_scales[0].bitcast(I32))
        xw_all = sb.tile([P, T], I32, name="xw_all", tag="stage_x", align_bytes=64)
        nc.sync.dma_start(xw_all[:], x_words[0].rearrange("p n t -> p (n t)").bitcast(I32))
        w1_late = staging.tile([P, PACK - 1, H], F32, name="w1_late", align_bytes=64, offset=ROW_BYTES)
        nc.sync.dma_start(w1_late[:], w1_rows[:, 1:])
        nc.sync.dma_start(lb_sb[:], lb)
        nc.sync.dma_start(la_sb[:], la)

        first, second, third, last = PLANE_ORDER
        w1_bf = sb.tile([P, PACK, P, PACK], BF16, name="w1_bf", align_bytes=64)
        early_src = w1_early[:, 0, :].rearrange("p (b t r) -> p t b r", t=PACK, r=RUN)
        early_dst = w1_bf[:, :, :, 0].rearrange("p t (b r) -> p t b r", r=RUN)
        nc.scalar.copy(early_dst[:, first, W1_SPLIT:], early_src[:, first, W1_SPLIT:])
        odd_planes = slice(last, PACK, third - last)
        nc.scalar.copy(early_dst[:, odd_planes], early_src[:, odd_planes])

        xs_picked = sb.tile([P, S], U8, name="xs_picked", align_bytes=64)
        nc.vector.tensor_copy(xs_picked[:], xs_all[:].indirect(offs_sb[:]))
        for q in range(4):
            rows = slice(scale_base + 4 * q, scale_base + 4 * q + 4)
            nc.scalar.dma_start(xs[32 * q : 32 * q + 4, :].bitcast(I32), xs_picked[rows, :].bitcast(I32))
        nc.vector.tensor_copy(early_dst[:, first, :W1_SPLIT], early_src[:, first, :W1_SPLIT])
        nc.vector.tensor_copy(early_dst[:, second], early_src[:, second])

        xw = sb.tile([P, S], U32, name="xw", align_bytes=64)
        for h in range(2):
            nc.vector.tensor_copy(
                xw[:, h * HALF : (h + 1) * HALF],
                xw_all[:].bitcast(U32).indirect(offs_sb[:, h * HALF // LIST_ROWS : (h + 1) * HALF // LIST_ROWS]),
            )

        late_src = w1_late[:].rearrange("p j (b t r) -> p t b r j", t=PACK, r=RUN)
        late_dst = w1_bf[:, :, :, 1:].rearrange("p t (b r) j -> p t b r j", r=RUN)
        nc.vector.tensor_copy(late_dst[:, first, :W1_SPLIT], late_src[:, first, :W1_SPLIT])
        nc.scalar.copy(late_dst[:, first, W1_SPLIT:], late_src[:, first, W1_SPLIT:])
        nc.vector.tensor_copy(late_dst[:, second], late_src[:, second])
        nc.scalar.copy(late_dst[:, third], late_src[:, third])
        nc.scalar.copy(late_dst[:, last], late_src[:, last])

        w1_codes, w1_scales = {}, {}
        for t in PLANE_ORDER:
            codes = sb.tile([P, P], U32, name="w1_codes%d" % t, align_bytes=64)
            scales = sb.tile([P, P], U8, name="w1_scales%d" % t, align_bytes=64)
            nc.vector.quantize_mx(
                out=codes[:].bitcast(FP8X4),
                scales=scales[:],
                in_=w1_bf[:, t].rearrange("p m j -> p (m j)"),
            )
            w1_codes[t] = codes[:]
            w1_scales[t] = scales[:]

        gates = sb.tile([P, 2, V], F32, name="gates", tag="stage_c", align_bytes=64)
        gate_a, gate_b = gates[:, 0, :], gates[:, 1, :]
        nc.sync.dma_start(gate_b, wb.rearrange("(b t r) v -> t b r v", t=PACK, r=RUN)[0])
        nc.sync.dma_start(gate_a, wa.rearrange("(b t r) v -> t b r v", t=PACK, r=RUN)[0])
        w2_raw = sb.tile([P, PACK, N], F32, name="w2_raw", tag="stage_x", align_bytes=64)
        w2_rows = w2.rearrange("(b t r) c -> t b r c", t=PACK, r=RUN)
        for t in range(PACK):
            nc.sync.dma_start(w2_raw[:, t, :], w2_rows[t])

        def first_product(t, cols, bank):
            acc = psum.tile([P, cols.stop - cols.start], F32, name="acc1", tag="bank%d" % bank)
            nc.tensor.matmul_mx(
                out=acc[:],
                lhsT=w1_codes[t].bitcast(FP8X4),
                lhsT_scale=w1_scales[t],
                rhs=xw[:, cols].bitcast(FP8X4),
                rhs_scale=xs[:, cols],
                start=True,
                stop=True,
            )
            return acc

        lo = slice(0, HALF)
        y = {}
        for t in PLANE_ORDER:
            y[t] = sb.tile([P, S], F32, name="y", tag="y%d" % t, align_bytes=64)
        pieces = (
            (lo, nc.vector.tensor_copy),
            (slice(HALF, HALF + P), nc.scalar.copy),
            (slice(HALF + P, S), nc.scalar.copy),
        )
        for bank, (cols, copy_out) in enumerate(pieces):
            acc = first_product(first, cols, bank)
            copy_out(y[first][:, cols], acc[:])

        w2_bf = sb.tile([P, N, PACK], BF16, name="w2_bf", align_bytes=64)

        def lay_out_w2(cols):
            nc.scalar.copy(
                w2_bf[:, cols].rearrange("p (c i) j -> p c j i", i=LINE),
                w2_raw[:, :, cols].rearrange("p j (c i) -> p c j i", i=LINE),
            )

        picked, z = {}, {}
        offsets = {"a": la_sb, "b": lb_sb}
        gate = {"a": gate_a, "b": gate_b}
        z_bf = [sb.tile([P, HALF, PACK], BF16, name="z_bf%d" % h, align_bytes=64) for h in range(2)]
        for t in PLANE_ORDER:
            width = 2 * S if t == first else S
            z[t] = reused.tile([P, width], F32, name="z%d" % t, align_bytes=64, offset=t * 8 * S)

        def empty_plane(t, bank, cols):
            acc = first_product(t, cols, bank)
            nc.scalar.copy(y[t][:, cols], acc[:])

        def fetch(route, t):
            picked[route, t] = sb.tile([P, V], F32, name="picked_%s%d" % (route, t), align_bytes=64)
            window = y[t][:].indirect(offsets[route][:])
            if (route, t) == ("b", first):
                cut = V // 2 // LIST_ROWS
                nc.vector.tensor_copy(picked[route, t][:, : V // 2], y[t][:].indirect(lb_sb[:, :cut]))
                nc.scalar.activation(picked[route, t][:, V // 2 :], y[t][:].indirect(lb_sb[:, cut:]), COPY)
            else:
                nc.scalar.activation(picked[route, t][:], window, COPY)

        def activate(t):
            active = sb.tile([P, V], F32, name="active%d" % t, align_bytes=64)
            nc.scalar.activation(active[:], picked["a", t][:], RELU)
            picked["a", t] = active

        def put(route, t):
            nc.vector.tensor_tensor(z[t][:].indirect(offsets[route][:]), picked[route, t][:], gate[route], MULT)

        def round_plane(copy, t, h, cols):
            copy(z_bf[h][:, cols, t], z[t][:, h * HALF + cols.start : h * HALF + cols.stop])

        q0, q1, both = slice(0, P), slice(P, HALF), slice(0, HALF)
        fetch("b", first)
        put("b", first)
        empty_plane(second, 3, slice(0, P))
        empty_plane(second, 4, slice(P, HALF))
        empty_plane(second, 5, slice(HALF, S))
        empty_plane(third, 6, slice(0, HALF))
        fetch("b", second)
        put("b", second)
        fetch("a", first)
        fetch("a", second)
        activate(first)
        put("a", first)
        activate(second)
        put("a", second)
        empty_plane(third, 7, slice(HALF, S))
        fetch("b", third)
        put("b", third)
        empty_plane(last, 0, slice(0, S))
        fetch("b", last)
        put("b", last)
        banks_used = 1
        lay_out_w2(slice(0, 2 * P - W2_LATE))
        fetch("a", third)
        lay_out_w2(slice(2 * P, 3 * P))
        activate(third)
        put("a", third)
        nc.scalar.copy(z[first][:, S:], z[second][:])
        fetch("a", last)
        pair = z[first][:].rearrange("p (t c) -> p c t", t=2)
        for h in range(2):
            nc.scalar.copy(z_bf[h][:, :, first : second + 1 : second - first], pair[:, h * HALF : (h + 1) * HALF])
        lay_out_w2(slice(3 * P, N))
        activate(last)
        put("a", last)
        lay_out_w2(slice(2 * P - W2_LATE, 2 * P))

        w2_scales = sb.tile([P, N], U8, name="w2_scales", align_bytes=64)

        def quantize_w2(codes, cols):
            nc.vector.quantize_mx(
                out=codes.bitcast(FP8X4), scales=w2_scales[:, cols], in_=w2_bf[:, cols].rearrange("p c j -> p (c j)")
            )

        w2_lower = sb.tile([P, N // 2], U32, name="w2_lower", align_bytes=64)
        quantize_w2(w2_lower[:], slice(0, N // 2))
        round_plane(nc.scalar.copy, third, 0, q0)
        round_plane(nc.scalar.copy, third, 0, q1)
        round_plane(nc.scalar.copy, third, 1, both)
        round_plane(nc.vector.tensor_copy, last, 0, q0)
        round_plane(nc.vector.tensor_copy, last, 0, q1)
        round_plane(nc.vector.tensor_copy, last, 1, slice(0, LAST_SPLIT))
        round_plane(nc.scalar.copy, last, 1, slice(LAST_SPLIT, HALF))

        z_codes = [sb.tile([P, HALF], U32, name="z_codes%d" % h, align_bytes=64) for h in range(2)]
        z_scales = [sb.tile([P, HALF], U8, name="z_scales%d" % h, align_bytes=64) for h in range(2)]

        def quantize_z(h, cols):
            nc.vector.quantize_mx(
                out=z_codes[h][:, cols].bitcast(FP8X4),
                scales=z_scales[h][:, cols],
                in_=z_bf[h][:, cols].rearrange("p c j -> p (c j)"),
            )

        quantize_z(0, q0)
        quantize_z(0, q1)
        quantize_z(1, both)
        w2_upper = reused.tile([P, N // 2], U32, name="w2_upper", align_bytes=64, offset=last * 8 * S)
        quantize_w2(w2_upper[:, :P], slice(2 * P, 3 * P))
        quantize_w2(w2_upper[:, P:], slice(3 * P, N))
        w2_codes = [w2_lower[:, :P], w2_lower[:, P:], w2_upper[:, :P], w2_upper[:, P:]]

        steps = [(0, 0, q0), (1, 0, q0), (0, 0, q1), (1, 0, q1), (0, 1, both), (1, 1, both)]
        steps.extend([(2, 0, both), (2, 1, both), (3, 0, both), (3, 1, q0), (3, 1, q1)])
        scalar_alone = 4
        banks = [(banks_used + n) % BANKS for n in range(len(steps))]
        banks[7], banks[8] = banks[8], banks[7]
        res = [sb.tile([P, S], F32, name="res%d" % r, align_bytes=64) for r in range(N // P)]
        for n, (r, h, cols) in enumerate(steps):
            bank = banks[n]
            acc = psum.tile([P, cols.stop - cols.start], F32, name="acc2", tag="bank%d" % bank)
            nc.tensor.matmul_mx(
                out=acc[:],
                lhsT=w2_codes[r].bitcast(FP8X4),
                lhsT_scale=w2_scales[:, r * P : (r + 1) * P],
                rhs=z_codes[h][:, cols].bitcast(FP8X4),
                rhs_scale=z_scales[h][:, cols],
                start=True,
                stop=True,
            )
            tokens = slice(h * HALF + cols.start, h * HALF + cols.stop)
            if n < scalar_alone or (n - scalar_alone) % 2 == 1:
                nc.scalar.copy(res[r][:, tokens], acc[:])
            else:
                nc.vector.tensor_copy(res[r][:, tokens], acc[:])
            width = (tokens.stop - tokens.start, HALF, S, S)[r]
            if tokens.stop % width == 0:
                stored = slice(tokens.stop - width, tokens.stop)
                nc.sync.dma_start(out[r * P : (r + 1) * P, stored], res[r][:, stored])
